import numpy as np, ml_dtypes
CORES = [24,25,26,27,28,29,30,31]
N = 8
BF = ml_dtypes.bfloat16
def gentries(a):
    return np.ascontiguousarray(a.reshape(8, 16, -1).transpose(0, 2, 1)).reshape(8, -1)
def gtable(e):
    e = np.asarray(e); return np.ascontiguousarray(e.reshape(8, -1, 16).transpose(0, 2, 1)).reshape(128, -1).astype(np.int32)
V, G, R, CAP, L, RO = 3200, 128, 512, 128, 2, 2
W = V + (N - 1) * G
def full(p):
    return np.concatenate([p, np.broadcast_to(np.arange(V, W), (N, 8, W - V))], axis=2).astype(np.int64)
def reach(t, p):
    m = t; q = p
    for i in range(L):
        m = np.maximum(m, np.take_along_axis(m, q[:, :, None, :], 3)); q = np.take_along_axis(q, q, 2)
    return m
def pointers(rng, stay):
    p = rng.integers(0, W, (N, 8, V))
    return np.where(rng.random((N, 8, V)) < stay, np.arange(V), p)
def base(rng):
    x = (256 * rng.random((N, 8, 16, W)) * rng.random((N, 8, 1, W))).astype(np.int32)
    return x, pointers(rng, 0.3), pointers(rng, 0.3), rng.integers(0, W, (N, 8, 16, R)), rng.integers(0, V, (N, 8, N - 1, G))
def both(x, up, lo):
    return reach(x, full(up))[..., :V], reach(x, full(lo))[..., :V]
def witness(rng, mu, ml):
    s = mu.shape; w = np.where(rng.random(s) < rng.random((N, 8, 1, V)), mu, ml) + rng.integers(-6, 7, s)
    w = w + np.where(rng.random((N, 8, 1, V)) < 0.3, rng.integers(-120, 121, s), 0)
    return np.minimum(np.maximum(w, 0), 255)
def bar(mu, ml, w, n):
    d = np.add.reduce(np.abs(mu - w), axis=2) + np.add.reduce(np.abs(ml - w), axis=2)
    return np.take_along_axis(np.sort(d, axis=2), V - 1 - n[:, :, None], 2)[:, :, 0]
def pack(x, w, th, up, lo, rl, snd):
    return {"x": np.ascontiguousarray(x.reshape(N, 128, W)).astype(np.float32).astype(BF), "w": np.ascontiguousarray(w.reshape(N, 128, V)).astype(np.float32).astype(BF),
            "th": np.repeat(th, 16, axis=1).reshape(N, 128, 1).astype(np.int32), "up": np.stack([gtable(a) for a in up]), "lo": np.stack([gtable(a) for a in lo]),
            "rl": np.ascontiguousarray(rl.reshape(N, 128, R)).astype(np.int32), "snd": np.stack([gtable(a.reshape(8, -1)) for a in snd])}
def setup_inputs(rng):
    x, up, lo, rl, snd = base(rng); mu, ml = both(x, up, lo); w = witness(rng, mu, ml)
    n = rng.choice(np.array([CAP // 4, CAP - 8, 2 * CAP, 4 * CAP]), (N, 8))
    return pack(x, w, bar(mu, ml, w, n), up, lo, rl, snd)
def setup_inputs_room(rng):
    x, up, lo, rl, snd = base(rng); mu = reach(x, full(up))[..., :V]
    n = rng.choice(np.array([0, 1, CAP - 1, CAP, CAP + 1, V]), (N, 8)); n[0] = (CAP, CAP + 1, V, CAP - 1, 1, 0, CAP, CAP + 1); n[1, 0] = CAP
    mark = np.argsort(rng.random((N, 8, V)), axis=2) < n[:, :, None]
    off = np.where(mark[:, :, None, :], rng.integers(20, 91, mu.shape), rng.integers(0, 4, mu.shape))
    return pack(x, np.where(mu < 128, mu + off, mu - off), rng.integers(100, 600, (N, 8)), up, up, rl, snd)
def setup_inputs_alike(rng):
    x, up, lo, rl, snd = base(rng); ends = np.array([0, 3, V - 1, V, W - 1])
    x = np.take_along_axis(rng.integers(0, 256, (N, 8, 16, 6)), rng.integers(0, 6, (N, 8, 1, W)), 3).astype(np.int32)
    up = pointers(rng, 0.6); lo = pointers(rng, 0.6)
    up[:, 1::2] = np.where(rng.random((N, 4, V)) < 0.5, rng.choice(ends, (N, 4, V)), up[:, 1::2]); lo[:, ::4] = rng.choice(ends, (N, 2, V))
    rl[:, 2:6] = np.tile(rl[:, 2:6, :4], (1, 1, 4, 1)); rl[:, 6] = rng.choice(ends, (N, 16, R)); rl[:, 7] = rl[:, 7, :1]
    snd[:, ::2] = rng.choice(np.array([0, 3, V - 2, V - 1]), (N, 4, N - 1, G))
    mu, ml = both(x, up, lo); w = witness(rng, mu, ml); n = rng.choice(np.array([CAP // 2, CAP, 2 * CAP]), (N, 8))
    return pack(x, w, bar(mu, ml, w, n), up, lo, rl, snd)
def setup_inputs_deep(rng):
    x, up, lo, rl, snd = base(rng)
    x = (rng.integers(0, 16, x.shape) + np.where(rng.random((N, 8, 1, W)) * 12 < 1, rng.integers(0, 240, x.shape), 0)).astype(np.int32)
    for c in (0, V - 1, V, W - 1): x[..., c] = rng.integers(0, 256, (N, 8, 16))
    up[:, ::2] = (np.arange(V) + 1) % V
    o = np.argsort(rng.random((N, 4, V)), axis=2); p = np.empty_like(o); np.put_along_axis(p, o, np.roll(o, -1, axis=2), 2); up[:, 1::2] = p
    lo = pointers(rng, 0.0); lo[:, ::3] = np.maximum(np.arange(V) - 1, 0); lo[:, 1, V - 1] = W - 1; lo[:, 2, 0] = V
    mu, ml = both(x, up, lo); w = witness(rng, mu, ml); n = rng.choice(np.array([CAP // 2, CAP, 3 * CAP]), (N, 8))
    return pack(x, w, bar(mu, ml, w, n), up, lo, rl, snd)
def setup_inputs_crowd(rng):
    x, up, lo, rl, snd = base(rng); own = np.arange(V); m = np.argsort(rng.random((N, 8, V)), axis=2); w = np.zeros((N, 8, 16, V), np.int64)
    lo[:, :2] = up[:, :2]; mark = own % 16 == rng.integers(0, 16, (N, 2, 1))
    mu = reach(x[:, :2], full(up)[:, :2])[..., :V]
    off = np.where(mark[:, :, None, :], rng.integers(20, 91, mu.shape), rng.integers(0, 4, mu.shape))
    w[:, :2] = np.where(mu < 128, mu + off, mu - off)
    for a in range(N):
        for g in (2, 3, 4, 5, 7):
            b = 37 if g < 4 else 1; n = CAP if g in (2, 7) else int(rng.choice(np.array([CAP, CAP + 1, V // 2])))
            big = np.flatnonzero(m[a, g] >= V - b); hit = m[a, g] < n
            x[a, g] = x[a, g] * 5 // 8; x[a, g][:, big] = rng.integers(201, 256, (16, b))
            if g == 7:
                zero = np.flatnonzero((m[a, g] >= V - 65) & (m[a, g] < V - 1)); x[a, g][:, zero] = 0; rl[a, g] = rng.choice(zero, (16, R))
            lo[a, g] = np.where(hit, rng.choice(big, V), own)
            go = hit & (g < 7)
            up[a, g] = np.where(go & ~np.isin(up[a, g], big), up[a, g], own)
            mine = x[a, g][:, :V]
            w[a, g] = np.where(go, (mine * rng.random(mine.shape)).astype(np.int64), mine)
            if g == 5:
                p = up[a, g].copy(); up[a, g] = lo[a, g]; lo[a, g] = p
    far = np.zeros((N, 8, 1, 1), bool); far[:, 6] = True; far[int(rng.integers(0, N))] = True
    x = np.where(far, 200 + x * 55 // 255, x); w = np.where(far, rng.integers(0, 31, w.shape), w)
    return pack(x, w, rng.integers(100, 600, (N, 8)), up, lo, rl, snd)
def setup_inputs_spread(rng):
    x, up, lo, rl, snd = base(rng)
    cs = np.exp2(8 * rng.random((N, 8, 1, W))) * (rng.random((N, 8, 1, W)) > 0.0625)
    x = np.minimum((cs * rng.random(x.shape)).astype(np.int32), 255)
    up = pointers(rng, rng.choice(np.array([0.0, 0.1, 0.5, 0.9]), (N, 8, 1))); lo = pointers(rng, rng.choice(np.array([0.0, 0.1, 0.5, 0.9]), (N, 8, 1)))
    mu, ml = both(x, up, lo)
    w = np.where(rng.random((N, 8, 1, 1)) < 0.5, witness(rng, mu, ml), np.minimum((cs[..., ::-1][..., :V] * rng.random(mu.shape)).astype(np.int32), 255))
    th = bar(mu, ml, w, rng.choice(np.array([0, 1, CAP, 3 * CAP, V - 1]), (N, 8)))
    th = np.where(rng.random((N, 8)) < 0.2, rng.choice(np.array([0, 8160]), (N, 8)), th)
    return pack(x, w, th, up, lo, rl, snd)
def check_inputs(d):
    bad = []
    for k, least, most in (("x", 0, 255), ("w", 0, 255), ("th", 0, 8160), ("up", 0, W - 1), ("lo", 0, W - 1), ("rl", 0, W - 1), ("snd", 0, V - 1)):
        a = np.asarray(d[k]).astype(np.float64)
        if not (np.min(a) >= least and np.max(a) <= most): bad.append("range of " + k)
        elif np.any(a != np.floor(a)): bad.append("whole numbers in " + k)
    t = np.asarray(d["th"]).reshape(-1, 16)
    if np.any(t != t[:, :1]): bad.append("th alike in a group")
    return bad
def reference(x, w, th, up, lo, rl, snd):
    t = x.astype(np.float32).astype(np.int32).reshape(N, 8, 16, W).copy(); z = w.astype(np.float32).astype(np.int32).reshape(N, 8, 16, V)
    lim = th.astype(np.int64).reshape(N, 8, 16)[:, :, 0]
    hi = full(np.stack([gentries(a) for a in up])); dn = full(np.stack([gentries(a) for a in lo]))
    rh = rl.astype(np.int64).reshape(N, 8, 16, R).copy(); sl = np.stack([gentries(a) for a in snd]).astype(np.int64).reshape(N, 8, N - 1, G)
    last = np.zeros(N, np.int64)
    for rnd in range(RO):
        mu = reach(t, hi); ml = reach(t, dn)
        y = np.concatenate([mu[:, :, :8], ml[:, :, 8:]], axis=2)
        du = np.add.reduce(np.abs(mu[..., :V] - z), axis=2); dl = np.add.reduce(np.abs(ml[..., :V] - z), axis=2)
        bad = du + dl > lim[:, :, None] + (last & 15)[:, None, None]
        last = np.add.reduce(bad.reshape(N, 8 * V).astype(np.int64), axis=1)
        for a in range(N):
            for g in range(8):
                v = np.flatnonzero(bad[a, g])[:CAP]
                if len(v) == 0: continue
                upper = du[a, g, v] >= dl[a, g, v]
                h = np.where(upper, hi[a, g, v], dn[a, g, v]) & (R - 1)
                can = rh[a, g][:, h]
                e = np.add.reduce(np.abs(y[a, g][:, can] - z[a, g][:, v][:, None, :]), axis=0)
                k = np.argmin(e, axis=0); c = can[k, np.arange(len(v))]
                hi[a, g, v[upper]] = c[upper]; dn[a, g, v[~upper]] = c[~upper]
                cls, first = np.unique(h, return_index=True)
                rh[a, g, k[first], cls] = v[first]
        if rnd < RO - 1:
            for a in range(N):
                for d in range(1, N):
                    q = (a - d) % N
                    t[a, :, :, V + (d - 1) * G:V + d * G] = np.take_along_axis(y[q], sl[q, :, d - 1][:, None, :], 2)
    return {"y": np.ascontiguousarray(y[..., :V]).reshape(N, 128, V).astype(np.float32).astype(BF), "up1": np.stack([gtable(a) for a in hi[..., :V]]).astype(np.float32),
            "lo1": np.stack([gtable(a) for a in dn[..., :V]]).astype(np.float32), "rl1": rh.reshape(N, 128, R).astype(np.float32)}

@@ -1,0 +1,488 @@
+from concourse.bass import DstId, RemoteDMATransfer
+from concourse.mybir import AluOpType, AxisListType, ActivationFunctionType
+
+V, W, NR = 3200, 4096, 8
+SPEC = {
+    "bfloat16": "xa 4096 xb 4096 wv 3216 m1u 4096 m1l 4096 mu 4096 ml 3200 win 4096 qu 3200 ql 3200 au 3200 al 3200 ft 512 rt 512 ht 456 "
+                "sb 896 nrow 128 c16 256 krow 128 jq 128 id1 128 idn 128 idk 128 ones 128 blk 128 mt 128 cs 144 g1 8 gp 8 gn 8 ca 200 cb 200 "
+                "c160 200 cw 16 rsk 128 k0 128 rsj 1024 bad 200 upp 208 sc 200 junk 1400 cmp 416 oh 128 s1 208 ne 200 lv 208 wa 128 "
+                "wt 128 ex 2048 yc 2048 ab 2048 oul 264 cr 272 same 264 dab 1024 dmn 1024 eq 144",
+    "float32": "zt 512 pt 512 h1 456 h2 456 rlw 640 thf 4 col 16 jp 128 t16 8 jc 8 jh 8 jk 8 dump 8 id8 128 idn32 128 blk32 128 tu 200 "
+               "duc 200 kt 208 tm 200 hs 208 acc 8 cf 128 sul 264 vm 128 vm2 128 tr 128 hj 8 nb 8 da 8 db 8 km 128 kn 128 pr 128 val 264 seg 272",
+    "int32": "ti 512 rli 512 sni 56 thi 4 bi 4 lsi 8",
+    "uint16": "l1 456 lp 456 l2 400 snu 56 lsu 8 cl 8 ll 14 wl 16 cu 128 dl 8",
+}
+SCRATCH = {"ps": ("psum", [128, 4096], "float32"), "qq": ("sbuf", [128, 2, 128], "bfloat16")}
+for _d, _s in SPEC.items():
+    _w = _s.split()
+    for _i in range(0, len(_w), 2):
+        SCRATCH[_w[_i]] = ("sbuf", [128, int(_w[_i + 1])], _d)
+SEMAPHORES = ["ev", "es", "ep", "eg", "arr", "sent"] + ["d%d" % i for i in range(40)]
+
+CH = [(0, 64), (64, 128), (128, 176), (176, 200)]
+CUT = CH[3][0]
+M16 = 1.5 * 2.0 ** 27
+M512 = 1.5 * 2.0 ** 32
+BIG = 1 << 23
+
+
+def rank_program(g, core, T, topo):
+    rank = T.rank_of(core)
+    if rank is None:
+        return
+    A, F = AluOpType, ActivationFunctionType
+    ve, se, pe = g.vector, g.scalar, g.tensor
+    queue = {"v": ve, "s": se, "p": pe, "g": g, "y": g.sync}
+    ops = []
+
+    def a(name, lo=0, hi=None, st=1, p=slice(None)):
+        hi = SCRATCH[name][1][1] if hi is None else hi
+        return (T[name][p, lo:hi:st] if st > 1 else T[name][p, lo:hi], [(name, lo, hi)])
+
+    def c1(name, i):
+        return a(name, i, i + 1)
+
+    def hbm(t, key=None):
+        return (t, [(key, 0, 1)] if key else [])
+
+    def bank(b, lo, hi, st=1):
+        return a("ps", 512 * b + lo, 512 * b + hi, st)
+
+    def ind(w_, o):
+        return (w_[0].indirect(o[0]), w_[1] + o[1])
+
+    def val(x):
+        return x[0] if isinstance(x, tuple) else x
+
+    def rng(*xs):
+        return [r for x in xs if isinstance(x, tuple) for r in x[1]]
+
+    def reg(e, calls, kind="c"):
+        ops.append({"e": e, "f": [c[0] for c in calls], "r": rng(*[x for c in calls for x in c[1]]),
+                    "w": rng(*[x for c in calls for x in c[2]]), "k": kind})
+
+    def ts(o, i, s1, o0, s2=None, o1=None):
+        if o1 is None:
+            reg("v", [(lambda: ve.tensor_scalar(o[0], i[0], val(s1), None, o0), [i, s1], [o])])
+        else:
+            reg("v", [(lambda: ve.tensor_scalar(o[0], i[0], val(s1), s2, o0, o1), [i, s1], [o])])
+
+    def tt(o, i, j, op, wr=None):
+        reg("v", [(lambda: ve.tensor_tensor(o[0], i[0], j[0], op), [i, j] + ([o] if wr else []), [wr or o])])
+
+    def cp(o, i):
+        reg("v", [(lambda: ve.tensor_copy(o[0], i[0]), [i], [o])])
+
+    def scan(o, d0, d1, o0, o1):
+        reg("v", [(lambda: ve.tensor_tensor_scan(o[0], d0[0], d1[0], 0.0, o0, o1), [d0, d1], [o])])
+
+    def red(o, i):
+        reg("v", [(lambda: ve.tensor_reduce(o[0], i[0], AxisListType.X, A.add), [i], [o])])
+
+    def actv(o, i, f=F.Identity, scale=1.0, bias=0.0, acc=None):
+        if acc is None:
+            return (lambda: se.activation(o[0], i[0], f, bias=val(bias), scale=val(scale)), [i, scale, bias], [o])
+        return (lambda: se.activation(o[0], i[0], f, bias=val(bias), scale=val(scale), accum_out=acc[0]), [i, scale, bias], [o, acc])
+
+    def act(*x, **k):
+        reg("s", [actv(*x, **k)])
+
+    def mm(o, l, r, s0, s1):
+        return (lambda: pe.matmul(o[0], l[0], r[0], s0, s1), [l, r], [o])
+
+    def grp(o, terms, s0=True, s1=True):
+        return [mm(o, l, r, s0 and i == 0, s1 and i == len(terms) - 1) for i, (l, r) in enumerate(terms)]
+
+    def wrap(o, src, first=True):
+        reg("p", grp(o, [(a("cs", 15 - r, 143 - r), src(r)) for r in range(16)], first))
+
+    def iota(o, pat, base=0, cm=0, whole=False):
+        if whole:
+            reg("g", [(lambda: g.iota(o[0], pat, base, cm), [], [o])])
+        else:
+            reg("g", [(lambda: g.iota(o[0], pat, base, cm, allow_small_or_imprecise_dtypes=True), [], [o])])
+
+    def fill(o, n, v):
+        iota(o, [[0, n]], v)
+
+    def sel(o, i, pat, op, fl, base, cm):
+        reg("g", [(lambda: g.affine_select(o[0], i[0], pat, op, fl, base, cm), [i], [o])])
+
+    def dma(e, pairs):
+        reg(e, [((o[0], i[0]), [i], [o]) for o, i in pairs], "d")
+
+    def ghosts(src):
+        for nm in ("m1u", "m1l", "mu"):
+            sel(a(nm, V, W), a(src, V, W), [[0, W - V]], A.is_ge, 0.0, 0, 0)
+
+    PF, RC, R85, MU_, ML_ = c1("col", 10), c1("col", 3), c1("col", 4), c1("col", 6), c1("col", 9)
+    I1, IN = a("id1"), a("idn")
+    qr, qh = (T.qq[:, 0, :], [("qq", 0, 128)]), (T.qq[:, 1, :], [("qq", 128, 256)])
+    WIN = (T.win[:], [("win0", 0, 1), ("win1", 0, 1)])
+
+    dma("y", [(a("ti", 0, 200), hbm(T.up[:])), (a("ti", 256, 456), hbm(T.lo[:]))])
+    dma("y", [(a("xa"), hbm(T.x[:])), (a("xb", 0, 512), hbm(T.x[:, 0:512]))])
+    dma("y", [(a("xb", 512, 1536), hbm(T.x[:, 512:1536]))])
+    iota(PF, [[0, 1]], 0, 1)
+    iota(a("nrow"), [[1, 128]])
+    iota(a("c16"), [[16, 256]])
+    iota(a("t16"), [[16, 8]])
+    fill(a("ca"), 200, -256)
+    reg("v", [(lambda: ve.memset(T.win[:], 0.0), [], [WIN])])
+    act(c1("col", 0), PF, bias=-7.5)
+    act(c1("col", 1), c1("col", 0), bias=M16)
+    act(c1("col", 2), c1("col", 1), bias=-M16)
+    act(RC, c1("col", 2), scale=-1.0, bias=PF)
+    act(R85, RC, bias=8.5)
+    act(c1("col", 5), RC, F.Sign, -1.0, 1.5)
+    act(c1("col", 7), RC, F.Abs, 1.0, -2.5)
+    act(a("jc"), a("t16"), bias=RC)
+    act(MU_, c1("col", 5), F.Relu)
+    act(c1("col", 8), c1("col", 7), F.Sign, -1.0, 1.0)
+    act(a("jh"), a("jc"), bias=0.5)
+    act(a("jk"), a("jc"), scale=1024.0)
+    act(a("dump"), a("jc"), bias=512.0)
+    act(ML_, c1("col", 8), F.Relu)
+    act(a("cb"), a("ca"), scale=0.0, bias=-8.5)
+    act(a("jq"), a("nrow"), scale=1.0 / 256)
+    ts(a("zt", 200, 256), a("c16", 200, 256), R85, A.add)
+    ts(a("zt", 456, 512), a("c16", 200, 256), R85, A.add)
+    ts(I1, a("nrow"), PF, A.is_equal)
+    ts(a("idk"), a("nrow"), PF, A.is_equal, 4096.0, A.mult)
+    ts(IN, a("nrow"), PF, A.is_equal, -1.0, A.mult)
+    ts(a("zt", 0, 200), a("ti", 0, 200), 8.5, A.add)
+    ts(a("zt", 256, 456), a("ti", 256, 456), 8.5, A.add)
+    glo, ghi = ([[-16, 8]], A.is_ge, 0.0, 0, 1), ([[16, 8]], A.is_ge, 0.0, 15, -1)
+    blo, bhi = ([[-16, 8], [0, 16]], A.is_ge, 0.0, 0, 1), ([[16, 8], [0, 16]], A.is_ge, 0.0, 15, -1)
+    diag = [[-1, 128]]
+    fill(a("cs"), 144, 0)
+    fill(a("ones"), 128, 1)
+    sel(a("g1"), a("ones", 0, 8), *glo)
+    sel(a("cs", 15, 128, 16), a("g1"), *ghi)
+    for nm, n, v in (("gp", 8, 32), ("gn", 8, -16), ("blk32", 128, 1), ("mt", 128, -1), ("id8", 128, 8), ("idn32", 128, -1), ("rsk", 128, 0),
+                     ("k0", 128, 0), ("c160", 200, 160)):
+        fill(a(nm), n, v)
+    ghosts("xa")
+    for nm in ("gp", "gn"):
+        sel(a(nm), a(nm), *glo)
+    sel(a("blk"), a("ones"), *blo)
+    sel(a("blk32"), a("blk32"), *blo)
+    sel(a("mt"), a("mt"), *bhi)
+    sel(a("id8"), a("id8"), diag, A.is_equal, 0.0, 0, 1)
+    sel(a("idn32"), a("idn32"), diag, A.is_equal, 0.0, 0, 1)
+    for nm in ("gp", "gn"):
+        sel(a(nm), a(nm), *ghi)
+    sel(a("blk"), a("blk"), *bhi)
+    sel(a("blk32"), a("blk32"), *bhi)
+    sel(a("mt"), a("mt"), diag, A.is_gt, 0.0, 0, 1)
+    iota(a("krow"), [[0, 8], [1, 16]])
+    sel(a("mt"), a("mt"), diag, A.not_equal, 256.0, 0, 1)
+    iota(a("jp"), [[1, 128]], 257)
+    iota(a("lsi"), [[16, 8]], 15, 0, True)
+    fill(a("rsk", 0, 128, 16), 8, BIG)
+    fill(a("k0", 0, 128, 16), 8, 1)
+    for nm, lo, v in (("cw", 0, 1600), ("cw", 8, 256), ("kt", 200, 0), ("hs", 200, 0), ("upp", 200, 0), ("cmp", 200, -25), ("cmp", 408, -25),
+                      ("wv", V, 0), ("wv", V + 8, 0), ("lv", 200, 0), ("s1", 0, 0), ("seg", 0, 0),
+                      ("oul", 128, 0), ("sul", 128, 0), ("cr", 0, -1), ("cr", 136, -1), ("eq", 8, 1)):
+        fill(a(nm, lo, lo + 8), 8, v)
+    fill(a("rlw", 512, 640), 128, 0)
+    for b in range(4):
+        iota(a("ex", 512 * b, 512 * b + 512), [[-1, 32], [0, 16]], 1 - 32 * b, 1)
+    for b in range(4):
+        sel(a("ex", 512 * b, 512 * b + 512), a("ex", 512 * b, 512 * b + 512), [[-1, 32], [0, 16]], A.is_equal, 0.0, -32 * b, 1)
+
+    cls = [lambda: scan(a("dmn"), a("rsj"), a("dab"), A.add, A.min),
+           lambda: tt(a("da"), a("hj"), a("dmn", 127, 1024, 128), A.subtract),
+           lambda: tt(a("db"), a("da"), a("dump"), A.min),
+           lambda: cp(a("dl"), a("db")),
+           lambda: tt(ind(a("rlw"), a("dl")), a("tr"), a("cf"), A.add, a("rlw"))]
+
+    for rnd in range(2):
+        xn, xo = ("xa", "xb") if rnd == 0 else ("xb", "xa")
+        n = 512 if rnd == 0 else 456
+        ts(a("ft", 0, n), a("zt", 0, n), M16, A.add, M16 + 16.0, A.subtract)
+        dma("y", [((T.win[j:128:16, :], [("win0", 0, 1)]), a("ft", 128 * j, 128 * j + 256)) for j in (0, 2)])
+        reg("p", [mm(bank(5, 0, n), IN, a("ft", 0, n), True, True)])
+        ts(a("l1"), a("zt", 0, 456), -8.5, A.add)
+        tt(a("rt", 0, n), bank(5, 0, n), a("zt", 0, n), A.add)
+        dma("y", [((T.win[j + 1:128:16, :], [("win1", 0, 1)]), a("rt", 128 * j, 128 * j + 256)) for j in (0, 2)])
+        reg("p", grp(bank(6, 0, 456), [(I1, a("ft", 0, 456)), (a("idk"), a("rt", 0, 456))]))
+        act(a("pt", 0, n), a("zt", 0, n), bias=-8.5)
+        act(a("h1"), a("zt", 0, 456), bias=-264.0)
+        act(a("h2"), a("h1"), bias=M512)
+        act(a("ht"), a("h2"), bias=-M512)
+        if rnd == 0:
+            act(a("xb", 1536, V), a("xa", 1536, V))
+
+        def first(tb, lo, hi, cut=None):
+            dst, off = ("m1u", "m1l")[tb], 256 * tb
+            tt(a(dst, 16 * lo, 16 * hi), ind(a(xn), a("l1", off + lo, off + hi)), a(xo, 16 * lo, 16 * hi), A.max)
+            if cut is not None:
+                dma("y", [(a(("mu", "ml")[tb], 16 * cut, 16 * hi), a(dst, 16 * cut, 16 * hi))])
+
+        def pilist():
+            ts(a("lp"), bank(6, 0, 456), 1.0 / 16, A.mult, -2176.0, A.add)
+
+        if rnd == 0:
+            pilist()
+        first(0, 0, 32)
+        if rnd == 1:
+            pilist()
+        first(0, 32, 96, 0)
+        if rnd == 0:
+            dma("y", [(a("wv", 0, V), hbm(T.w[:]))])
+        first(0, 96, 200, 96)
+        fu, fl, ru, rl_, hu, hl = [a(nm, o, o + 200) for nm in ("ft", "rt", "ht") for o in (0, 256)]
+        reg("p", grp(bank(7, 0, 200), [(I1, fu), (I1, ru), (I1, hl), (IN, hu), (IN, fl), (IN, rl_)])
+            + grp(bank(7, 200, 400), [(I1, fl), (I1, rl_), (I1, a("ca")), (I1, a("cb")), (IN, hl)]))
+        first(1, 0, 112, 0)
+        if rnd == 0:
+            dma("y", [(c1("thi", 0), hbm(T.th[:])), (a("sni"), hbm(T.snd[:])), (a("rli"), hbm(T.rl[:]))])
+        first(1, 112, 200, 112)
+
+        def twice(tb, hf):
+            nm, o = "qu" if tb == 0 else "ql", 256 * tb + 100 * hf
+            act(a(nm, 1600 * hf, 1600 * hf + 1600), ind(WIN, a("lp", o, o + 100)), scale=(MU_, ML_)[tb])
+            wrap(bank(4 + tb, 100 * hf, 100 * hf + 100), lambda r: a(nm, 1600 * hf + r, 1600 * hf + 1600, 16))
+
+        def qlist(tb):
+            ts(a("l2", 200 * tb, 200 * tb + 200), bank(4 + tb, 0, 200), -8.5, A.add)
+
+        def second(tb, i):
+            lo, hi = CH[i]
+            src, dst = (("m1u", "mu"), ("m1l", "ml"))[tb]
+            tt(a(dst, 16 * lo, 16 * hi), ind(a(src), a("l2", 200 * tb + lo, 200 * tb + hi)), a(dst, 16 * lo, 16 * hi), A.max)
+            pp = [(x, min(x + 512, 16 * hi)) for x in range(16 * lo, 16 * hi, 512)]
+            reg("p", [mm(bank(2 * (i % 2) + j, 0, z - x), IN, a("wv", x, z), True, False) for j, (x, z) in enumerate(pp)])
+            reg("p", [mm(bank(2 * (i % 2) + j, 0, z - x), I1, a(dst, x, z), False, True) for j, (x, z) in enumerate(pp)])
+
+        def dist(tb, i):
+            lo, hi = CH[i]
+            nm = "au" if tb == 0 else "al"
+            act(a(nm, 16 * lo, 16 * hi), bank(2 * (i % 2), 0, 16 * (hi - lo)), F.Abs)
+            wrap(bank(6 if (tb, i) == (1, 3) else 4 + tb, lo, hi), lambda r: a(nm, 16 * lo + r, 16 * hi, 16))
+
+        def halves(lo, hi):
+            dma("y", [(a("mu", lo, hi, p=slice(16 * q + 8, 16 * q + 16)), a("ml", lo, hi, p=slice(16 * q + 8, 16 * q + 16))) for q in range(8)])
+
+        twice(0, 0); twice(0, 1); twice(1, 0)
+        qlist(0)
+        second(0, 0)
+        twice(1, 1)
+        second(0, 1); dist(0, 0)
+        second(0, 2); dist(0, 1)
+        second(0, 3); dist(0, 2)
+        qlist(1)
+        if rnd == 0:
+            cp(c1("thf", 0), c1("thi", 0))
+        second(1, 0); dist(0, 3)
+        second(1, 1); dist(1, 0)
+        second(1, 2); dist(1, 1)
+        halves(0, 16 * CUT)
+        second(1, 3); dist(1, 2)
+        halves(16 * CUT, V)
+        dist(1, 3)
+        if rnd == 1:
+            cls[0]()
+        ts(a("tu"), bank(4, 0, 200), c1("thf", rnd), A.subtract, -1.0, A.mult)
+        if rnd == 1:
+            cls[1]()
+        cp(a("duc"), bank(4, 0, 200))
+        if rnd == 0:
+            cp(a("rlw", 0, 512), a("rli"))
+            cp(a("snu"), a("sni"))
+            cp(a("lsu"), a("lsi"))
+        else:
+            cls[2]()
+            cls[3]()
+            dma("y", [(hbm(T.y[:], "out0"), a("mu", 0, V))])
+
+        tt(a("bad", 0, CUT), bank(5, 0, CUT), a("tu", 0, CUT), A.is_gt)
+        tt(a("upp", 0, CUT), bank(5, 0, CUT), a("duc", 0, CUT), A.is_le)
+        tt(a("bad", CUT, 200), bank(6, CUT, 200), a("tu", CUT, 200), A.is_gt)
+        reg("p", [mm(bank(0, 0, 200), a("blk"), a("bad"), True, True), mm(bank(0, 200, 400), a("mt"), a("bad"), True, True)])
+        tt(a("upp", CUT, 200), bank(6, CUT, 200), a("duc", CUT, 200), A.is_le)
+        tt(a("tm"), bank(7, 0, 200), a("upp", 0, 200), A.mult)
+        scan(a("sc"), bank(0, 0, 200), a("c160"), A.add, A.min)
+        reg("p", [mm(bank(1, 128, 144), I1, a("cw"), True, False)])
+        if rnd == 0:
+            reg("p", [mm(bank(4, 200, 400), a("ones"), a("bad"), True, True)])
+        reg("s", [actv(a("junk", 200 * t, 200 * t + 200), a("sc"), F.Sign, -1.0, c1("jh", t), c1("acc", t)) for t in range(6)])
+        tt(a("hs", 0, 200), bank(7, 200, 400), a("tm"), A.add)
+        ts(a("cmp", 0, 200), a("sc"), c1("jc", 6), A.is_le, 2.0, A.mult)
+        ts(a("cmp", 208, 408), a("sc"), c1("jc", 7), A.is_le, 2.0, A.mult)
+        tt(a("kt", 0, 200), bank(0, 200, 400), a("sc"), A.add)
+        red(c1("acc", 6), a("cmp", 0, 208))
+        red(c1("acc", 7), a("cmp", 208, 416))
+        if rnd == 1:
+            cls[4]()
+        ts(a("cl"), a("acc"), 0.5, A.mult, 100.0, A.add)
+        reg("p", [mm(bank(1, 128, 136), a("id8"), a("acc"), False, False)])
+        tt(a("oh"), ind(a("kt"), a("cl")), a("jp"), A.is_equal)
+        tt(qh, ind(a("hs"), a("cl")), a("oh"), A.mult)
+        ts(qr, a("oh"), RC, A.mult)
+        wrap(bank(1, 128, 144), lambda r: (T.qq[:, :, r:128:16], [("qq", 0, 256)]), False)
+
+        def slot_rows():
+            act(a("cr", 8, 136), ind(a("c16"), a("cl")))
+            act(a("cr", 144, 272), ind(a("c16"), a("cl")))
+            act(a("sul", 0, 128), ind(a("pt", 0, 256), a("cl")))
+            act(a("sul", 136, 264), ind(a("pt", 256, 512), a("cl")))
+
+        def slot_mm():
+            reg("p", grp(bank(5, 0, 128), [(a("blk"), qr), (I1, a("cr", 8, 136))]) + [mm(bank(5, 128, 256), a("blk"), a("oh"), True, True)])
+
+        def old_mm():
+            reg("p", [mm(bank(6, 0, 264), a("idn32"), a("sul"), True, False)])
+
+        if rnd == 0:
+            act(a("sb"), ind(a("mu"), a("snu")))
+            reg("g", [(None, [a("sb")], [])], "x")
+            fill(a("rsj"), 1024, 0)
+            fill(a("rsj", 0, 1024, 128), 8, BIG)
+        else:
+            slot_rows()
+        ts(a("s1", 8, 208), a("sc"), 128.0, A.min)
+        tt(a("ne"), a("s1", 8, 208), a("s1", 7, 207), A.not_equal)
+        tt(a("lv", 0, 200), a("ne"), a("s1", 8, 208), A.mult)
+        cp(a("wl"), bank(1, 128, 144))
+        reg("p", grp(bank(4, 0, 128), [(I1, a("jq")), (a("blk"), qh)]))
+
+        cp(a("cu"), ind(a("rlw"), a("wl", 8, 16)))
+        act(a("wa"), ind(a("wv"), a("wl", 0, 8)))
+        tt(a("hj"), bank(1, 136, 144), a("jk"), A.add)
+        wrap(bank(5, 256, 269), lambda r: a("lv", r, 208, 16))
+        reg("p", [mm(bank(5, 300, 428), a("wa"), IN, True, True)])
+        act(a("nb"), bank(1, 136, 144), scale=-262144.0, bias=67108864.0)
+        act(a("wt"), bank(5, 300, 428))
+        if rnd == 1:
+            old_mm()
+        yc = [a("yc", 512 * b, 512 * b + 512) for b in range(4)]
+        src = [ind(a("mu"), a("cu", 32 * b, 32 * b + 32)) for b in range(4)]
+        act(yc[0], src[0])
+        cp(yc[2], src[2])
+        act(yc[1], src[1])
+        cp(yc[3], src[3])
+        reg("p", [mm(bank(7, 0, 128), I1, a("krow"), True, False)])
+        for b in (2, 0, 3, 1):
+            reg("p", [mm(bank(b, 0, 512), a("wt"), a("ex", 512 * b, 512 * b + 512), True, False)])
+        for b in (2, 0, 3, 1):
+            reg("p", [mm(bank(b, 0, 512), I1, yc[b], False, True)])
+        reg("p", [mm(bank(7, k, 128, 16), a("yc", k, 2048, 16), a("gn"), False, False) for k in range(16)])
+        for b in range(2):
+            act(a("ab", 512 * b, 512 * b + 512), bank(b, 0, 512), F.Relu)
+            ts(a("ab", 1024 + 512 * b, 1536 + 512 * b), bank(2 + b, 0, 512), 0.0, A.max)
+        reg("p", [mm(bank(7, k, 128, 16), a("ab", k, 2048, 16), a("gp"), False, k == 15) for k in range(16)])
+        act(a("cf"), ind(a("rlw"), a("wl", 8, 16)))
+        ts(a("ll", 0, 13), bank(5, 256, 269), 1.0 / 16, A.mult, 7.0, A.add)
+        one = bank(1, 0, 128)
+        reg("p", [mm(one, a("k0"), I1, True, False)])
+        if rnd == 0:
+            slot_rows()
+            slot_mm()
+            old_mm()
+            act(a("junk", 1200, 1400), bank(4, 200, 400), acc=c1("thf", 2))
+        tt(a("oul", 0, 128), ind(a("upp"), a("cl")), a("oh"), A.mult)
+        tt(a("oul", 136, 264), a("oh"), a("oul", 0, 128), A.subtract)
+        if rnd == 1:
+            slot_mm()
+            tt(a("same"), a("cr", 8, 272), a("cr", 7, 271), A.is_equal)
+        reg("s", [actv(a("dab", 128 * t, 128 * t + 128), bank(4, 0, 128), F.Abs, 262144.0, c1("nb", t)) for t in range(8)])
+        scan(a("km"), a("rsk"), bank(7, 0, 128), A.add, A.min)
+        scan(a("kn"), a("rsk"), bank(7, 0, 128), A.add, A.min)
+        tt(a("eq", 16, 144), ind(a("km"), a("lsu")), a("kn"), A.is_equal)
+        reg("p", grp(one, [(a("eq", 16, 144), I1), (a("eq", 15, 143), IN)], False))
+        tt(a("vm"), bank(5, 0, 128), a("cf"), A.subtract)
+        tt(a("pr"), one, a("cf"), A.mult)
+        reg("p", [mm(bank(6, 0, 128), a("blk32"), a("pr"), False, False), mm(bank(6, 136, 264), a("blk32"), a("pr"), False, True)])
+        tt(a("vm2"), bank(5, 128, 256), a("vm"), A.mult)
+        if rnd == 0:
+            tt(a("same"), a("cr", 8, 272), a("cr", 7, 271), A.is_equal)
+        else:
+            cls[0]()
+        tt(a("val"), bank(6, 0, 264), a("oul"), A.mult)
+        if rnd == 1:
+            cls[1]()
+        tt(a("tr"), one, a("vm2"), A.mult)
+        if rnd == 1:
+            cls[2]()
+        scan(a("seg", 8, 272), a("same"), a("val"), A.mult, A.add)
+        if rnd == 0:
+            cp(c1("bi", 0), c1("thf", 2))
+            tt(a("zt", 0, 208), ind(a("seg", 0, 136), a("ll", 0, 13)), a("zt", 0, 208), A.add)
+            ts(c1("bi", 1), c1("bi", 0), 15, A.bitwise_and)
+            tt(a("zt", 256, 464), ind(a("seg", 136, 272), a("ll", 0, 13)), a("zt", 256, 464), A.add)
+            tt(c1("thf", 1), c1("bi", 1), c1("thf", 0), A.add)
+            reg("y", [(None, [], [a("xb", V, W)])], "a")
+            ghosts("xb")
+        else:
+            cls[3]()
+            tt(a("pt", 0, 208), ind(a("seg", 0, 136), a("ll", 0, 13)), a("pt", 0, 208), A.add)
+            dma("y", [(hbm(T.up1[:], "out1"), a("pt", 0, 200))])
+            cls[4]()
+            dma("y", [(hbm(T.rl1[:], "out3"), a("rlw", 0, 512))])
+            tt(a("pt", 256, 464), ind(a("seg", 136, 272), a("ll", 0, 13)), a("pt", 256, 464), A.add)
+            dma("s", [(hbm(T.lo1[:], "out2"), a("pt", 256, 456))])
+    reg("y", [(None, [hbm(None, "out%d" % i) for i in range(4)], [])], "n")
+    reg("g", [(None, [], [])], "e")
+
+    def exchange():
+        eng = topo.engines(core, T.cores[(rank + 1) % NR])
+        far, near = list(eng[0::2]), list(eng[1::2])
+        trs = []
+        for d in range(1, NR):
+            dst = T.cores[(rank + d) % NR]
+            pool = far if topo.die(dst) != topo.die(core) else near
+            mask = (1 << pool.pop()) | (1 << pool.pop())
+            rid, pid = topo.addr(dst)[0:2]
+            trs.append(RemoteDMATransfer(dst_ids=[DstId(rid=rid, pnc=pid)], dma_engine_mask=mask, remote_sem=T.sem.arr,
+                                         src=T.sb[:, 128 * (d - 1):128 * d], dst=T.xb[:, V + 128 * (d - 1):V + 128 * d]))
+        g.remote_dma_fused(trs, local_sem=T.sem.sent)
+
+    hist = {}
+    know = {e: {} for e in queue}
+    for i, o in enumerate(ops):
+        e = o["e"]
+        use = [(r, False) for r in o["r"]] + [(r, True) for r in o["w"]]
+        use = [((nm, lo // 512 * 512, -(-hi // 512) * 512), wr) if nm == "ps" else ((nm, lo, hi), wr) for (nm, lo, hi), wr in use]
+        need = {}
+        for (nm, lo, hi), wr in use:
+            for l2, h2, w2, j in hist.get(nm, []):
+                src = ops[j]["src"]
+                if l2 < hi and lo < h2 and ((src != e) if nm == "ps" else (wr or w2)) and not (src == "p" and e == "p"):
+                    need[src] = max(need.get(src, -1), j)
+        o["waits"] = []
+        for src, j in sorted(need.items(), key=lambda t: -t[1]):
+            if know[e].get(src, -1) < j:
+                o["waits"].append(j)
+                ops[j]["inc"] = True
+                for s2, j2 in list(ops[j]["know"].items()) + [(src, j)]:
+                    know[e][s2] = max(know[e].get(s2, -1), j2)
+        o["src"] = e if o["k"] == "c" else "z%d" % i
+        o["know"] = dict(know[e]) if o["k"] != "a" else {}
+        for (nm, lo, hi), wr in use:
+            hist.setdefault(nm, []).append((lo, hi, wr, i))
+    count = {e: 0 for e in queue}
+    nd = 0
+    for o in ops:
+        e, q = o["e"], queue[o["e"]]
+        for j in o["waits"]:
+            q.wait_ge(*ops[j]["sig"])
+        if o["k"] == "c":
+            ins = [f() for f in o["f"]][-1]
+            if o.get("inc"):
+                count[e] += 1
+                ins.then_inc(T.sem["e" + e], 1)
+                o["sig"] = (T.sem["e" + e], count[e])
+        elif o["k"] == "d":
+            sem = T.sem["d%d" % nd]
+            nd += 1
+            for dst, src in o["f"]:
+                q.dma_start(dst, src).then_inc(sem, 16)
+            o["sig"] = (sem, 16 * len(o["f"]))
+        elif o["k"] == "a":
+            o["sig"] = (T.sem.arr, 2 * (NR - 1))
+        elif o["k"] == "x":
+            exchange()
+        elif o["k"] == "e":
+            g.wait_ge(T.sem.sent, 2 * (NR - 1))

@@ -2,28 +2,34 @@ from concourse.bass import DstId, RemoteDMATransfer
 from concourse.mybir import AluOpType, AxisListType, ActivationFunctionType
 
 V, W, NR = 3200, 4096, 8
+RS = 272
+LO = 16 * RS
 SPEC = {
-    "bfloat16": "xa 4096 xb 4096 wv 3216 m1u 4096 m1l 4096 mu 4096 ml 3200 win 4096 qu 3200 ql 3200 au 3200 al 3200 ft 512 rt 512 ht 456 "
-                "sb 896 nrow 128 c16 256 krow 128 jq 128 id1 128 idn 128 idk 128 ones 128 blk 128 mt 128 cs 144 g1 8 gp 8 gn 8 ca 200 cb 200 "
-                "c160 200 cw 16 rsk 128 k0 128 rsj 1024 bad 200 upp 208 sc 200 junk 1400 cmp 416 oh 128 s1 208 ne 200 lv 208 wa 128 "
-                "wt 128 ex 2048 yc 2048 ab 2048 oul 264 cr 272 same 264 dab 1024 dmn 1024 eq 144",
-    "float32": "zt 512 pt 512 h1 456 h2 456 rlw 640 thf 4 col 16 jp 128 t16 8 jc 8 jh 8 jk 8 dump 8 id8 128 idn32 128 blk32 128 tu 200 "
-               "duc 200 kt 208 tm 200 hs 208 acc 8 cf 128 sul 264 vm 128 vm2 128 tr 128 hj 8 nb 8 da 8 db 8 km 128 kn 128 pr 128 val 264 seg 272",
-    "int32": "ti 512 rli 512 sni 56 thi 4 bi 4 lsi 8",
-    "uint16": "l1 456 lp 456 l2 400 snu 56 lsu 8 cl 8 ll 14 wl 16 cu 128 dl 8",
+    "bfloat16": "xa 4096 xb 4096 wv 3328 m1 12800 mu 7552 wb 8704 qb 6400 ad 6400 ft 544 rt 544 ht 544 sb 1792 nrow 208 krow 128 jq 128 "
+                "id1 128 idn 128 idk 128 i16 128 ones 128 half 128 blk 128 mt 128 s1b 128 s2b 128 d1 128 d2 128 cs 144 cs2 144 g1 8 gp 8 gn 8 "
+                "ca 200 cb 200 cd 200 c160 208 cw 16 ee 32 sv 16 rsk 128 rsj 1024 bad 208 low 208 sc 208 junk 1456 cmp 432 oh 128 wa 128 wt 128 "
+                "xv 128 pv 128 crow 128 ex 2048 dab 1024 dmn 1024 eq 128 lw 128 vb 128 hs 208",
+    "float32": "zt 544 pt 472 c16 72 rlw 640 thf 8 col 24 jp 128 t16 8 jc 8 jh 8 dump 8 l1m 128 l2m 128 ow 9480 tu 200 duc 200 kt 208 tm 200 "
+               "acc 8 cf 128 vm 128 tr 128 nb 8 hj 8 da 8 db 8 km 128 ks 128 rr 128 val 128",
+    "int32": "ti 400 rli 512 sni 56 thi 4 lsi 8",
+    "uint16": "l1 400 lp 472 l2 400 snu 56 lsu 8 cl 8 wl 16 sl 32 cu 128 dl 8 cc 8",
 }
-SCRATCH = {"ps": ("psum", [128, 4096], "float32"), "qq": ("sbuf", [128, 2, 128], "bfloat16")}
+SCRATCH = {"ps": ("psum", [128, 4096], "float32"), "qq": ("sbuf", [128, 5, 128], "bfloat16")}
 for _d, _s in SPEC.items():
     _w = _s.split()
     for _i in range(0, len(_w), 2):
         SCRATCH[_w[_i]] = ("sbuf", [128, int(_w[_i + 1])], _d)
 SEMAPHORES = ["ev", "es", "ep", "eg", "arr", "sent"] + ["d%d" % i for i in range(40)]
 
-CH = [(0, 64), (64, 128), (128, 176), (176, 200)]
-CUT = CH[3][0]
+SEC = [(0, 0, 64), (0, 64, 128), (0, 128, 200), (1, 0, 56), (1, 56, 120), (1, 120, 176), (1, 176, 200)]
+SLOT = [0, 1024, 2048, 3072, 4096, 5120, 6016, 6400]
 M16 = 1.5 * 2.0 ** 27
 M512 = 1.5 * 2.0 ** 32
+HB = 66048
 BIG = 1 << 23
+ALL = 0xFFFF
+YC, AB, ML = LO, LO + 2048, 2 * LO
+FULL = 7
 
 
 def rank_program(g, core, T, topo):
@@ -35,18 +41,28 @@ def rank_program(g, core, T, topo):
     queue = {"v": ve, "s": se, "p": pe, "g": g, "y": g.sync}
     ops = []
 
-    def a(name, lo=0, hi=None, st=1, p=slice(None)):
+    def a(name, lo=0, hi=None, st=1):
         hi = SCRATCH[name][1][1] if hi is None else hi
-        return (T[name][p, lo:hi:st] if st > 1 else T[name][p, lo:hi], [(name, lo, hi)])
+        return (T[name][:, lo:hi:st] if st > 1 else T[name][:, lo:hi], [(name, lo, hi, ALL)])
+
+    def part(name, j, lo, hi):
+        return (T[name][j:128:16, lo:hi], [(name, lo, hi, 1 << j)])
+
+    def top(name, n):
+        return (T[name][0:n, :], a(name)[1])
 
     def c1(name, i):
         return a(name, i, i + 1)
 
     def hbm(t, key=None):
-        return (t, [(key, 0, 1)] if key else [])
+        return (t, [(key, 0, 1, ALL)] if key else [])
 
     def bank(b, lo, hi, st=1):
         return a("ps", 512 * b + lo, 512 * b + hi, st)
+
+    def qrow(i, n=1, r=None):
+        ap = T.qq[:, i, :] if r is None else T.qq[:, i:i + n, r:128:16]
+        return (ap, [("qq", 128 * i, 128 * (i + n), ALL)])
 
     def ind(w_, o):
         return (w_[0].indirect(o[0]), w_[1] + o[1])
@@ -65,19 +81,29 @@ def rank_program(g, core, T, topo):
         if o1 is None:
             reg("v", [(lambda: ve.tensor_scalar(o[0], i[0], val(s1), None, o0), [i, s1], [o])])
         else:
-            reg("v", [(lambda: ve.tensor_scalar(o[0], i[0], val(s1), s2, o0, o1), [i, s1], [o])])
+            reg("v", [(lambda: ve.tensor_scalar(o[0], i[0], val(s1), val(s2), o0, o1), [i, s1, s2], [o])])
 
-    def tt(o, i, j, op, wr=None):
-        reg("v", [(lambda: ve.tensor_tensor(o[0], i[0], j[0], op), [i, j] + ([o] if wr else []), [wr or o])])
+    def tt(o, i, j, op):
+        reg("v", [(lambda: ve.tensor_tensor(o[0], i[0], j[0], op), [i, j], [o])])
 
     def cp(o, i):
         reg("v", [(lambda: ve.tensor_copy(o[0], i[0]), [i], [o])])
+
+    def scatter(w_, o, i, j=None):
+        out = w_[0].indirect(o[0])
+        if j is None:
+            reg("v", [(lambda: ve.tensor_copy(out, i[0]), [i, o], [w_])])
+        else:
+            reg("v", [(lambda: ve.tensor_tensor(out, i[0], j[0], A.add), [i, j, o], [w_])])
 
     def scan(o, d0, d1, o0, o1):
         reg("v", [(lambda: ve.tensor_tensor_scan(o[0], d0[0], d1[0], 0.0, o0, o1), [d0, d1], [o])])
 
     def red(o, i):
         reg("v", [(lambda: ve.tensor_reduce(o[0], i[0], AxisListType.X, A.add), [i], [o])])
+
+    def zero(o):
+        reg("v", [(lambda: ve.memset(o[0], 0.0), [], [o])])
 
     def actv(o, i, f=F.Identity, scale=1.0, bias=0.0, acc=None):
         if acc is None:
@@ -93,8 +119,8 @@ def rank_program(g, core, T, topo):
     def grp(o, terms, s0=True, s1=True):
         return [mm(o, l, r, s0 and i == 0, s1 and i == len(terms) - 1) for i, (l, r) in enumerate(terms)]
 
-    def wrap(o, src, first=True):
-        reg("p", grp(o, [(a("cs", 15 - r, 143 - r), src(r)) for r in range(16)], first))
+    def wrap(o, src, s0=True, s1=True, by="cs"):
+        reg("p", grp(o, [(a(by, 15 - r, 143 - r), src(r)) for r in range(16)], s0, s1))
 
     def iota(o, pat, base=0, cm=0, whole=False):
         if whole:
@@ -111,318 +137,421 @@ def rank_program(g, core, T, topo):
     def dma(e, pairs):
         reg(e, [((o[0], i[0]), [i], [o]) for o, i in pairs], "d")
 
-    def ghosts(src):
-        for nm in ("m1u", "m1l", "mu"):
-            sel(a(nm, V, W), a(src, V, W), [[0, W - V]], A.is_ge, 0.0, 0, 0)
+    PF, RC, R85, MK, MR, MR2, RRS, UP, UPB, UP256, SG = [c1("col", i) for i in range(11)]
+    tmp = [c1("col", i) for i in range(12, 20)]
+    I1, IN, I16 = a("id1"), a("idn"), a("i16")
+    qo, qh, qr, ql, qp = [qrow(i) for i in range(5)]
+    nr = a("nrow", 0, 128)
 
-    PF, RC, R85, MU_, ML_ = c1("col", 10), c1("col", 3), c1("col", 4), c1("col", 6), c1("col", 9)
-    I1, IN = a("id1"), a("idn")
-    qr, qh = (T.qq[:, 0, :], [("qq", 0, 128)]), (T.qq[:, 1, :], [("qq", 128, 256)])
-    WIN = (T.win[:], [("win0", 0, 1), ("win1", 0, 1)])
+    def tab(nm, tb, n=RS):
+        return a(nm, RS * tb, RS * tb + n)
 
-    dma("y", [(a("ti", 0, 200), hbm(T.up[:])), (a("ti", 256, 456), hbm(T.lo[:]))])
-    dma("y", [(a("xa"), hbm(T.x[:])), (a("xb", 0, 512), hbm(T.x[:, 0:512]))])
-    dma("y", [(a("xb", 512, 1536), hbm(T.x[:, 512:1536]))])
+    def wrow(j, tb):
+        return part("wb", j, LO * tb, LO * tb + LO)
+
+    def owrows(tb):
+        return part("ow", FULL, V * tb, V * tb + V)
+
+    dma("y", [(a("ti", 0, 200), hbm(T.up[:])), (a("ti", 200, 400), hbm(T.lo[:]))])
+    dma("y", [(a("xa"), hbm(T.x[:]))])
     iota(PF, [[0, 1]], 0, 1)
-    iota(a("nrow"), [[1, 128]])
-    iota(a("c16"), [[16, 256]])
+    iota(a("nrow"), [[1, 208]])
+    iota(a("c16"), [[16, RS - 200]], V)
     iota(a("t16"), [[16, 8]])
-    fill(a("ca"), 200, -256)
-    reg("v", [(lambda: ve.memset(T.win[:], 0.0), [], [WIN])])
-    act(c1("col", 0), PF, bias=-7.5)
-    act(c1("col", 1), c1("col", 0), bias=M16)
-    act(c1("col", 2), c1("col", 1), bias=-M16)
-    act(RC, c1("col", 2), scale=-1.0, bias=PF)
+    zero(a("wb", 0, LO // 2))
+    zero(a("wb", LO // 2, LO))
+    act(tmp[0], PF, bias=-7.5)
+    act(tmp[1], tmp[0], bias=M16)
+    act(tmp[2], tmp[1], bias=-M16)
+    act(RC, tmp[2], scale=-1.0, bias=PF)
     act(R85, RC, bias=8.5)
-    act(c1("col", 5), RC, F.Sign, -1.0, 1.5)
-    act(c1("col", 7), RC, F.Abs, 1.0, -2.5)
-    act(a("jc"), a("t16"), bias=RC)
-    act(MU_, c1("col", 5), F.Relu)
-    act(c1("col", 8), c1("col", 7), F.Sign, -1.0, 1.0)
-    act(a("jh"), a("jc"), bias=0.5)
-    act(a("jk"), a("jc"), scale=1024.0)
-    act(a("dump"), a("jc"), bias=512.0)
-    act(ML_, c1("col", 8), F.Relu)
-    act(a("cb"), a("ca"), scale=0.0, bias=-8.5)
-    act(a("jq"), a("nrow"), scale=1.0 / 256)
-    ts(a("zt", 200, 256), a("c16", 200, 256), R85, A.add)
-    ts(a("zt", 456, 512), a("c16", 200, 256), R85, A.add)
-    ts(I1, a("nrow"), PF, A.is_equal)
-    ts(a("idk"), a("nrow"), PF, A.is_equal, 4096.0, A.mult)
-    ts(IN, a("nrow"), PF, A.is_equal, -1.0, A.mult)
-    ts(a("zt", 0, 200), a("ti", 0, 200), 8.5, A.add)
-    ts(a("zt", 256, 456), a("ti", 256, 456), 8.5, A.add)
+    act(a("zt", 200, RS), a("c16"), bias=R85)
+    act(a("zt", RS + 200, 2 * RS), a("c16"), bias=R85)
+    act(a("wb", LO, LO + LO // 2), a("wb", 0, LO // 2))
+    act(tmp[3], RC, F.Sign, -1.0, 1.5)
+    act(tmp[4], RC, F.Sign, -1.0, 7.5)
+    act(tmp[5], RC, F.Relu, 1.0, -1.0)
+    act(MK, tmp[3], F.Relu)
+    ts(IN, nr, PF, A.is_equal, -1.0, A.mult)
+    ts(I1, nr, PF, A.is_equal)
+    ts(a("idk"), nr, PF, A.is_equal, float(LO), A.mult)
+    fill(a("wb", LO + LO // 2, 2 * LO), LO // 2, 0)
+    fill(a("cs"), 144, 0)
+    fill(a("ones"), 128, 1)
     glo, ghi = ([[-16, 8]], A.is_ge, 0.0, 0, 1), ([[16, 8]], A.is_ge, 0.0, 15, -1)
     blo, bhi = ([[-16, 8], [0, 16]], A.is_ge, 0.0, 0, 1), ([[16, 8], [0, 16]], A.is_ge, 0.0, 15, -1)
     diag = [[-1, 128]]
-    fill(a("cs"), 144, 0)
-    fill(a("ones"), 128, 1)
     sel(a("g1"), a("ones", 0, 8), *glo)
     sel(a("cs", 15, 128, 16), a("g1"), *ghi)
-    for nm, n, v in (("gp", 8, 32), ("gn", 8, -16), ("blk32", 128, 1), ("mt", 128, -1), ("id8", 128, 8), ("idn32", 128, -1), ("rsk", 128, 0),
-                     ("k0", 128, 0), ("c160", 200, 160)):
+
+    def parts(tb):
+        ts(tab("zt", tb, 200), a("ti", 200 * tb, 200 * tb + 200), 8.5, A.add)
+        ts(tab("ft", tb), tab("zt", tb), M16, A.add, M16 + 16.0, A.subtract)
+        reg("p", [mm(bank(5 - tb, 0, RS), IN, tab("ft", tb), True, True)])
+        if tb == 0:
+            cp(a("l1"), a("ti"))
+        tt(tab("rt", tb), bank(5 - tb, 0, RS), tab("zt", tb), A.add)
+        dma("y", [(wrow(0, tb), tab("ft", tb)), (wrow(1, tb), tab("rt", tb))])
+
+    def place_mm(tb):
+        reg("p", grp(bank(3 - tb, 0, 200), [(I1, tab("ft", tb, 200)), (a("idk"), tab("rt", tb, 200))]))
+
+    def place(tb):
+        ts(tab("lp", tb, 200), bank(3 - tb, 0, 200), 1.0 / 16, A.mult, -8.5 * RS, A.add)
+
+    def classes():
+        fu, fl, ru, rl_, hu, hl = [tab(nm, tb, 200) for nm in ("ft", "rt", "ht") for tb in (0, 1)]
+        reg("p", grp(bank(7, 256, 456), [(I1, fl), (I1, rl_), (I1, hu), (IN, hl), (IN, fu), (IN, ru)])
+            + grp(bank(6, 256, 456), [(I1, fu), (I1, ru), (I1, a("ca")), (I1, a("cb")), (I1, a("cd")), (IN, hu)]))
+
+    act(UP, tmp[4], F.Relu)
+    act(UPB, tmp[4], scale=-256.0)
+    act(MR, tmp[5], scale=M512 - M16, bias=M16)
+    act(MR2, tmp[5], scale=M512 - M16 - HB, bias=M16)
+    act(UP256, UP, scale=256.0)
+    act(RRS, RC, scale=float(RS))
+    act(SG, PF, F.Sign, -1.0, 63.5)
+    act(a("jc"), a("t16"), bias=RC)
+    act(a("jh"), a("jc"), bias=0.5)
+    act(a("ee", 8, 16), a("jc"), scale=1024.0, bias=-127 * 1024.0)
+    act(a("dump"), a("jc"), bias=256.0)
+    act(I16, I1, scale=16.0)
+    parts(0)
+    place_mm(0)
+    place(0)
+    parts(1)
+    place_mm(1)
+    place(1)
+    dma("y", [(a("xb", 1536, V), hbm(T.x[:, 1536:V]))])
+    act(a("cb"), a("ft", 0, 200), scale=0.0, bias=-8.5)
+    act(a("xb", 0, 512), a("xa", 0, 512))
+    act(a("ht"), a("ft"), bias=65800.0)
+    act(a("xb", 512, 1536), a("xa", 512, 1536))
+
+    def ghosts(src, *to):
+        for nm, o in to:
+            sel(a(nm, o + V, o + W), a(src, V, W), [[0, W - V]], A.is_ge, 0.0, 0, 0)
+
+    def spread(b):
+        sel(a("ex", 512 * b, 512 * b + 512), a("ex", 512, 1024), [[-1, 32], [0, 16]], A.is_equal, 0.0, -32 * b, 1)
+
+    fill(a("ca"), 200, -256)
+    fill(a("cd"), 200, HB)
+    classes()
+    ghosts("xa", ("m1", 0), ("m1", ML))
+    for nm, n, v in (("mt", 128, -1), ("rsk", 128, 0), ("c160", 208, 160)):
         fill(a(nm), n, v)
-    ghosts("xa")
-    for nm in ("gp", "gn"):
-        sel(a(nm), a(nm), *glo)
+    fill(a("wv", V, V + 128), 128, 0)
     sel(a("blk"), a("ones"), *blo)
-    sel(a("blk32"), a("blk32"), *blo)
     sel(a("mt"), a("mt"), *bhi)
-    sel(a("id8"), a("id8"), diag, A.is_equal, 0.0, 0, 1)
-    sel(a("idn32"), a("idn32"), diag, A.is_equal, 0.0, 0, 1)
-    for nm in ("gp", "gn"):
-        sel(a(nm), a(nm), *ghi)
     sel(a("blk"), a("blk"), *bhi)
-    sel(a("blk32"), a("blk32"), *bhi)
     sel(a("mt"), a("mt"), diag, A.is_gt, 0.0, 0, 1)
     iota(a("krow"), [[0, 8], [1, 16]])
     sel(a("mt"), a("mt"), diag, A.not_equal, 256.0, 0, 1)
     iota(a("jp"), [[1, 128]], 257)
     iota(a("lsi"), [[16, 8]], 15, 0, True)
     fill(a("rsk", 0, 128, 16), 8, BIG)
-    fill(a("k0", 0, 128, 16), 8, 1)
-    for nm, lo, v in (("cw", 0, 1600), ("cw", 8, 256), ("kt", 200, 0), ("hs", 200, 0), ("upp", 200, 0), ("cmp", 200, -25), ("cmp", 408, -25),
-                      ("wv", V, 0), ("wv", V + 8, 0), ("lv", 200, 0), ("s1", 0, 0), ("seg", 0, 0),
-                      ("oul", 128, 0), ("sul", 128, 0), ("cr", 0, -1), ("cr", 136, -1), ("eq", 8, 1)):
+    for nm, lo, v in (("cw", 0, 256), ("cw", 8, 0), ("ee", 16, 0), ("bad", 200, 1), ("low", 200, 0), ("hs", 200, 256), ("cmp", 208, -26), ("cmp", 424, -26)):
         fill(a(nm, lo, lo + 8), 8, v)
     fill(a("rlw", 512, 640), 128, 0)
-    for b in range(4):
-        iota(a("ex", 512 * b, 512 * b + 512), [[-1, 32], [0, 16]], 1 - 32 * b, 1)
-    for b in range(4):
-        sel(a("ex", 512 * b, 512 * b + 512), a("ex", 512 * b, 512 * b + 512), [[-1, 32], [0, 16]], A.is_equal, 0.0, -32 * b, 1)
+    iota(a("s1b"), [[0, 64], [-2, 2]], 1)
+    iota(a("s2b"), [[0, 64], [1, 2]])
+    for side in (blo, bhi):
+        sel(a("s1b"), a("s1b"), *side)
+        sel(a("s2b"), a("s2b"), *side)
+    iota(a("d1"), [[0, 32], [-248, 2], [15, 2]], -8, 1)
+    iota(a("d2"), [[0, 64], [17, 2]])
+    ghosts("xa", ("mu", 0))
+    fill(a("ex", 512, 1024), 512, 1)
+    spread(2)
+    spread(0)
 
-    cls = [lambda: scan(a("dmn"), a("rsj"), a("dab"), A.add, A.min),
-           lambda: tt(a("da"), a("hj"), a("dmn", 127, 1024, 128), A.subtract),
-           lambda: tt(a("db"), a("da"), a("dump"), A.min),
-           lambda: cp(a("dl"), a("db")),
-           lambda: tt(ind(a("rlw"), a("dl")), a("tr"), a("cf"), A.add, a("rlw"))]
+    def first(rnd, tb, lo, hi, cut=None):
+        xn, xo = ("xa", "xb") if rnd == 0 else ("xb", "xa")
+        tt(a("m1", ML * tb + 16 * lo, ML * tb + 16 * hi), ind(a(xn), a("l1", 200 * tb + lo, 200 * tb + hi)), a(xo, 16 * lo, 16 * hi), A.max)
+        if cut is not None:
+            again(tb, cut, hi)
+
+    def again(tb, lo, hi):
+        dma("y", [(a("mu", LO * tb + 16 * lo, LO * tb + 16 * hi), a("m1", ML * tb + 16 * lo, ML * tb + 16 * hi))])
+
+    def twice(tb, hf):
+        o = V * tb + 1600 * hf
+        act(a("qb", o, o + 1600), ind(a("wb", LO * tb, LO * tb + LO), a("lp", RS * tb + 100 * hf, RS * tb + 100 * hf + 100)), scale=MK)
+
+    def twice_mm(tb, hf):
+        o = V * tb + 1600 * hf
+        wrap(bank(7 - tb, 100 * hf, 100 * hf + 100), lambda r: a("qb", o + r, o + 1600, 16))
+
+    def qlist(tb):
+        ts(a("l2", 200 * tb, 200 * tb + 200), bank(7 - tb, 0, 200), -8.5, A.add)
+
+    def cuts(i):
+        out, x = [], SLOT[i]
+        while x < SLOT[i + 1]:
+            z = min(SLOT[i + 1], x + 512 - (x - SLOT[i]) % 512, V if x < V else 2 * V)
+            out.append((1024 * (i % 3) + x - SLOT[i], x, z - x))
+            x = z
+        return out
+
+    def minus_w(i):
+        reg("p", [mm(a("ps", o, o + n), IN, a("wv", x % V, x % V + n), o % 512 == 0, False) for o, x, n in cuts(i)])
+
+    def second(i):
+        tb, lo, hi = SEC[i]
+        o = a("mu", LO * tb + 16 * lo, LO * tb + 16 * hi)
+        tt(o, ind(a("m1", ML * tb, ML * tb + W), a("l2", 200 * tb + lo, 200 * tb + hi)), o, A.max)
+
+    def plus_m(i):
+        cs_ = cuts(i)
+        reg("p", [mm(a("ps", o, o + n), I1, a("mu", x + (LO - V) * (x // V), x + (LO - V) * (x // V) + n), False,
+                     j == len(cs_) - 1 or cs_[j + 1][0] % 512 == 0) for j, (o, x, n) in enumerate(cs_)])
+
+    def absd(i):
+        act(a("ad", SLOT[i], SLOT[i + 1]), a("ps", 1024 * (i % 3), 1024 * (i % 3) + SLOT[i + 1] - SLOT[i]), F.Abs)
+
+    def dist(i):
+        tb, lo, hi = SEC[i]
+        wrap(bank(7 - tb, lo, hi), lambda r: a("ad", V * tb + 16 * lo + r, V * tb + 16 * hi, 16))
+
+    def halves(lo, hi):
+        dma("y", [(part("mu", j, lo, hi), part("mu", j, LO + lo, LO + hi)) for j in range(8, 16)])
+
+    first(0, 0, 0, 32)
+    first(0, 1, 0, 32)
+    dma("y", [(a("wv", 0, V), hbm(T.w[:]))])
+    first(0, 0, 32, 96, 0)
+    first(0, 1, 32, 96)
+    first(0, 0, 96, 200, 96)
+    dma("y", [(c1("thi", 0), hbm(T.th[:])), (a("sni"), hbm(T.snd[:]))])
+    first(0, 1, 96, 200, 0)
 
     for rnd in range(2):
-        xn, xo = ("xa", "xb") if rnd == 0 else ("xb", "xa")
-        n = 512 if rnd == 0 else 456
-        ts(a("ft", 0, n), a("zt", 0, n), M16, A.add, M16 + 16.0, A.subtract)
-        dma("y", [((T.win[j:128:16, :], [("win0", 0, 1)]), a("ft", 128 * j, 128 * j + 256)) for j in (0, 2)])
-        reg("p", [mm(bank(5, 0, n), IN, a("ft", 0, n), True, True)])
-        ts(a("l1"), a("zt", 0, 456), -8.5, A.add)
-        tt(a("rt", 0, n), bank(5, 0, n), a("zt", 0, n), A.add)
-        dma("y", [((T.win[j + 1:128:16, :], [("win1", 0, 1)]), a("rt", 128 * j, 128 * j + 256)) for j in (0, 2)])
-        reg("p", grp(bank(6, 0, 456), [(I1, a("ft", 0, 456)), (a("idk"), a("rt", 0, 456))]))
-        act(a("pt", 0, n), a("zt", 0, n), bias=-8.5)
-        act(a("h1"), a("zt", 0, 456), bias=-264.0)
-        act(a("h2"), a("h1"), bias=M512)
-        act(a("ht"), a("h2"), bias=-M512)
-        if rnd == 0:
-            act(a("xb", 1536, V), a("xa", 1536, V))
-
-        def first(tb, lo, hi, cut=None):
-            dst, off = ("m1u", "m1l")[tb], 256 * tb
-            tt(a(dst, 16 * lo, 16 * hi), ind(a(xn), a("l1", off + lo, off + hi)), a(xo, 16 * lo, 16 * hi), A.max)
-            if cut is not None:
-                dma("y", [(a(("mu", "ml")[tb], 16 * cut, 16 * hi), a(dst, 16 * cut, 16 * hi))])
-
-        def pilist():
-            ts(a("lp"), bank(6, 0, 456), 1.0 / 16, A.mult, -2176.0, A.add)
-
-        if rnd == 0:
-            pilist()
-        first(0, 0, 32)
+        for tb, hf in ((0, 0), (0, 1), (1, 0), (1, 1)):
+            twice(tb, hf)
+            if rnd == 1 and (tb, hf) == (0, 0):
+                for t2 in (0, 1):
+                    act(tab("pt", t2, 200), bank(4 + t2, 0, 200), bias=-8.5)
+                dma("y", [(owrows(t2), tab("pt", t2, 200)) for t2 in (0, 1)])
+        twice_mm(0, 0)
         if rnd == 1:
-            pilist()
-        first(0, 32, 96, 0)
-        if rnd == 0:
-            dma("y", [(a("wv", 0, V), hbm(T.w[:]))])
-        first(0, 96, 200, 96)
-        fu, fl, ru, rl_, hu, hl = [a(nm, o, o + 200) for nm in ("ft", "rt", "ht") for o in (0, 256)]
-        reg("p", grp(bank(7, 0, 200), [(I1, fu), (I1, ru), (I1, hl), (IN, hu), (IN, fl), (IN, rl_)])
-            + grp(bank(7, 200, 400), [(I1, fl), (I1, rl_), (I1, a("ca")), (I1, a("cb")), (IN, hl)]))
-        first(1, 0, 112, 0)
-        if rnd == 0:
-            dma("y", [(c1("thi", 0), hbm(T.th[:])), (a("sni"), hbm(T.snd[:])), (a("rli"), hbm(T.rl[:]))])
-        first(1, 112, 200, 112)
-
-        def twice(tb, hf):
-            nm, o = "qu" if tb == 0 else "ql", 256 * tb + 100 * hf
-            act(a(nm, 1600 * hf, 1600 * hf + 1600), ind(WIN, a("lp", o, o + 100)), scale=(MU_, ML_)[tb])
-            wrap(bank(4 + tb, 100 * hf, 100 * hf + 100), lambda r: a(nm, 1600 * hf + r, 1600 * hf + 1600, 16))
-
-        def qlist(tb):
-            ts(a("l2", 200 * tb, 200 * tb + 200), bank(4 + tb, 0, 200), -8.5, A.add)
-
-        def second(tb, i):
-            lo, hi = CH[i]
-            src, dst = (("m1u", "mu"), ("m1l", "ml"))[tb]
-            tt(a(dst, 16 * lo, 16 * hi), ind(a(src), a("l2", 200 * tb + lo, 200 * tb + hi)), a(dst, 16 * lo, 16 * hi), A.max)
-            pp = [(x, min(x + 512, 16 * hi)) for x in range(16 * lo, 16 * hi, 512)]
-            reg("p", [mm(bank(2 * (i % 2) + j, 0, z - x), IN, a("wv", x, z), True, False) for j, (x, z) in enumerate(pp)])
-            reg("p", [mm(bank(2 * (i % 2) + j, 0, z - x), I1, a(dst, x, z), False, True) for j, (x, z) in enumerate(pp)])
-
-        def dist(tb, i):
-            lo, hi = CH[i]
-            nm = "au" if tb == 0 else "al"
-            act(a(nm, 16 * lo, 16 * hi), bank(2 * (i % 2), 0, 16 * (hi - lo)), F.Abs)
-            wrap(bank(6 if (tb, i) == (1, 3) else 4 + tb, lo, hi), lambda r: a(nm, 16 * lo + r, 16 * hi, 16))
-
-        def halves(lo, hi):
-            dma("y", [(a("mu", lo, hi, p=slice(16 * q + 8, 16 * q + 16)), a("ml", lo, hi, p=slice(16 * q + 8, 16 * q + 16))) for q in range(8)])
-
-        twice(0, 0); twice(0, 1); twice(1, 0)
+            classes()
+        twice_mm(0, 1)
         qlist(0)
-        second(0, 0)
-        twice(1, 1)
-        second(0, 1); dist(0, 0)
-        second(0, 2); dist(0, 1)
-        second(0, 3); dist(0, 2)
-        qlist(1)
         if rnd == 0:
-            cp(c1("thf", 0), c1("thi", 0))
-        second(1, 0); dist(0, 3)
-        second(1, 1); dist(1, 0)
-        second(1, 2); dist(1, 1)
-        halves(0, 16 * CUT)
-        second(1, 3); dist(1, 2)
-        halves(16 * CUT, V)
-        dist(1, 3)
+            dma("y", [(a("rli"), hbm(T.rl[:]))])
+            dma("y", [(wrow(2, tb), tab("ht", tb)) for tb in (0, 1)])
+            twice_mm(1, 0)
+        for i in range(3):
+            minus_w(i)
         if rnd == 1:
-            cls[0]()
-        ts(a("tu"), bank(4, 0, 200), c1("thf", rnd), A.subtract, -1.0, A.mult)
-        if rnd == 1:
-            cls[1]()
-        cp(a("duc"), bank(4, 0, 200))
+            twice_mm(1, 0)
+        for i in range(7):
+            if i == 3:
+                qlist(1)
+                if rnd == 0:
+                    cp(c1("thf", 0), c1("thi", 0))
+                    cp(a("snu"), a("sni"))
+                    act(a("sb", 896, 1792), ind(a("mu", 0, V), a("snu")), scale=UP, bias=UPB)
+            second(i)
+            plus_m(i)
+            if i == 0:
+                twice_mm(1, 1)
+            if 0 < i < 5:
+                minus_w(i + 2)
+            for j in {1: [0], 2: [1], 4: [2], 5: [3], 6: [4, 5]}.get(i, []):
+                dist(j)
+            absd(i)
+            if i == 6:
+                act(a("tu"), bank(7, 0, 200), scale=-1.0, bias=c1("thf", rnd))
+                act(a("duc"), bank(7, 0, 200))
+            if i >= 5:
+                halves(*((0, 16 * SEC[6][1]), (16 * SEC[6][1], V))[i - 5])
+        dist(6)
+        if rnd == 0:
+            tt(a("sb", 896, 1792), ind(a("mu", LO, LO + V), a("snu")), a("sb", 896, 1792), A.min)
+            ts(a("sb", 0, 896), a("sb", 896, 1792), UP256, A.add)
+            reg("g", [(None, [a("sb", 0, 896)], [])], "x")
+            spread(3)
+            spread(1)
+            fill(a("m1", W, LO), LO - W, 0)
+            fill(a("rsj"), 1024, -1024)
+            fill(a("rsj", 0, 1024, 128), 8, BIG)
+            reg("y", [(None, [], [a("xb", V, W)])], "a")
+            act(a("gn"), a("cs", 15, 128, 16), scale=-16.0)
+            act(a("gp"), a("cs", 15, 128, 16), scale=32.0)
+            act(a("l1m"), a("s1b"), scale=-1.0)
+            act(a("l2m"), a("s2b"), scale=-1.0)
+            act(a("half"), a("ones"), scale=0.5)
+        else:
+            dma("y", [(hbm(T.y[:], "out0"), a("mu", 0, V))])
+            act(a("cs2"), a("cs"), scale=200.0)
+            for f in rhyme:
+                f()
+
+        tt(a("bad", 0, 200), bank(6, 0, 200), a("tu"), A.is_gt)
+        reg("p", [mm(bank(0, 0, 208), a("blk"), a("bad"), True, True)])
+        reg("p", [mm(bank(1, 0, 208), a("mt"), a("bad"), True, True)])
+        tt(a("low", 0, 200), bank(6, 0, 200), a("duc"), A.is_gt)
+        scan(a("sc"), bank(0, 0, 208), a("c160"), A.add, A.min)
+        if rnd == 0:
+            reg("p", [mm(bank(4, 200, 400), a("ones"), a("bad", 0, 200), True, True)])
+        reg("s", [actv(a("junk", 208 * t, 208 * t + 208), a("sc"), F.Sign, -1.0, c1("jh", t), c1("acc", t)) for t in range(6)])
+        tt(a("tm"), bank(7, 256, 456), a("low", 0, 200), A.mult)
+        ts(a("cmp", 0, 208), a("sc"), c1("jc", 6), A.is_le, 2.0, A.mult)
+        ts(a("cmp", 216, 424), a("sc"), c1("jc", 7), A.is_le, 2.0, A.mult)
+        tt(a("kt"), bank(1, 0, 208), a("sc"), A.add)
+        red(c1("acc", 6), a("cmp", 0, 216))
+        red(c1("acc", 7), a("cmp", 216, 432))
+        tt(a("hs", 0, 200), bank(6, 256, 456), a("tm"), A.add)
+        if rnd == 0:
+            cp(a("lsu"), a("lsi"))
+        reg("p", [mm(bank(7, 0, 16), I1, a("cw"), True, False)])
+        CW = a("ee", 24, 32) if rnd == 0 else a("ee", 0, 8)
+        ts(a("cl"), a("acc"), 0.5, A.mult, 104.0, A.add)
+        act(CW, a("acc"), scale=0.5, bias=104.0)
+        reg("p", [mm(bank(7, 8, 16), I16, CW, False, False)])
+        tt(a("oh"), ind(a("kt"), a("cl")), a("jp"), A.is_equal)
+        act(a("sv", 0, 8), a("acc"), F.Sign, 1.0, -191.0)
+        act(qr, a("oh"), scale=RC)
+        tt(qh, ind(a("hs"), a("cl")), a("oh"), A.mult)
+        wrap(bank(7, 0, 16), lambda r: qrow(1, 2, r), False)
+        tt(a("lw"), ind(a("low"), a("cl")), a("oh"), A.mult)
+        act(a("crow"), ind(a("nrow"), a("cl")))
+        SV = a("sv", 8, 16)
         if rnd == 0:
             cp(a("rlw", 0, 512), a("rli"))
-            cp(a("snu"), a("sni"))
-            cp(a("lsu"), a("lsi"))
+            act(ql, a("lw"), scale=float(LO))
+            act(qp, a("oh"), scale=RRS)
+            act(SV, a("sv", 0, 8), scale=28.0, bias=28.0)
         else:
-            cls[2]()
-            cls[3]()
-            dma("y", [(hbm(T.y[:], "out0"), a("mu", 0, V))])
-
-        tt(a("bad", 0, CUT), bank(5, 0, CUT), a("tu", 0, CUT), A.is_gt)
-        tt(a("upp", 0, CUT), bank(5, 0, CUT), a("duc", 0, CUT), A.is_le)
-        tt(a("bad", CUT, 200), bank(6, CUT, 200), a("tu", CUT, 200), A.is_gt)
-        reg("p", [mm(bank(0, 0, 200), a("blk"), a("bad"), True, True), mm(bank(0, 200, 400), a("mt"), a("bad"), True, True)])
-        tt(a("upp", CUT, 200), bank(6, CUT, 200), a("duc", CUT, 200), A.is_le)
-        tt(a("tm"), bank(7, 0, 200), a("upp", 0, 200), A.mult)
-        scan(a("sc"), bank(0, 0, 200), a("c160"), A.add, A.min)
-        reg("p", [mm(bank(1, 128, 144), I1, a("cw"), True, False)])
+            act(qo, a("lw"), scale=float(V))
+            act(SV, a("sv", 0, 8), scale=3136.0, bias=3136.0)
+        reg("p", [mm(bank(4, 0, 128), a("blk"), qh, True, True)])
+        cp(a("wl"), bank(7, 0, 16))
         if rnd == 0:
-            reg("p", [mm(bank(4, 200, 400), a("ones"), a("bad"), True, True)])
-        reg("s", [actv(a("junk", 200 * t, 200 * t + 200), a("sc"), F.Sign, -1.0, c1("jh", t), c1("acc", t)) for t in range(6)])
-        tt(a("hs", 0, 200), bank(7, 200, 400), a("tm"), A.add)
-        ts(a("cmp", 0, 200), a("sc"), c1("jc", 6), A.is_le, 2.0, A.mult)
-        ts(a("cmp", 208, 408), a("sc"), c1("jc", 7), A.is_le, 2.0, A.mult)
-        tt(a("kt", 0, 200), bank(0, 200, 400), a("sc"), A.add)
-        red(c1("acc", 6), a("cmp", 0, 208))
-        red(c1("acc", 7), a("cmp", 208, 416))
+            reg("p", [mm(bank(6, 8, 32), I1, a("ee", 8, 32), True, False)])
+            wrap(bank(6, 8, 32), lambda r: qrow(1, 3, r), False, False)
+        else:
+            reg("p", [mm(bank(6, 0, 16), I1, a("ee", 0, 16), True, False)])
+            wrap(bank(6, 0, 16), lambda r: qrow(0, 2, r), False, False)
+
+        cp(a("cu"), ind(a("rlw"), a("wl", 0, 8)))
         if rnd == 1:
-            cls[4]()
-        ts(a("cl"), a("acc"), 0.5, A.mult, 100.0, A.add)
-        reg("p", [mm(bank(1, 128, 136), a("id8"), a("acc"), False, False)])
-        tt(a("oh"), ind(a("kt"), a("cl")), a("jp"), A.is_equal)
-        tt(qh, ind(a("hs"), a("cl")), a("oh"), A.mult)
-        ts(qr, a("oh"), RC, A.mult)
-        wrap(bank(1, 128, 144), lambda r: (T.qq[:, :, r:128:16], [("qq", 0, 256)]), False)
-
-        def slot_rows():
-            act(a("cr", 8, 136), ind(a("c16"), a("cl")))
-            act(a("cr", 144, 272), ind(a("c16"), a("cl")))
-            act(a("sul", 0, 128), ind(a("pt", 0, 256), a("cl")))
-            act(a("sul", 136, 264), ind(a("pt", 256, 512), a("cl")))
-
-        def slot_mm():
-            reg("p", grp(bank(5, 0, 128), [(a("blk"), qr), (I1, a("cr", 8, 136))]) + [mm(bank(5, 128, 256), a("blk"), a("oh"), True, True)])
-
-        def old_mm():
-            reg("p", [mm(bank(6, 0, 264), a("idn32"), a("sul"), True, False)])
-
-        if rnd == 0:
-            act(a("sb"), ind(a("mu"), a("snu")))
-            reg("g", [(None, [a("sb")], [])], "x")
-            fill(a("rsj"), 1024, 0)
-            fill(a("rsj", 0, 1024, 128), 8, BIG)
-        else:
-            slot_rows()
-        ts(a("s1", 8, 208), a("sc"), 128.0, A.min)
-        tt(a("ne"), a("s1", 8, 208), a("s1", 7, 207), A.not_equal)
-        tt(a("lv", 0, 200), a("ne"), a("s1", 8, 208), A.mult)
-        cp(a("wl"), bank(1, 128, 144))
-        reg("p", grp(bank(4, 0, 128), [(I1, a("jq")), (a("blk"), qh)]))
-
-        cp(a("cu"), ind(a("rlw"), a("wl", 8, 16)))
-        act(a("wa"), ind(a("wv"), a("wl", 0, 8)))
-        tt(a("hj"), bank(1, 136, 144), a("jk"), A.add)
-        wrap(bank(5, 256, 269), lambda r: a("lv", r, 208, 16))
+            act(a("jq"), bank(4, 0, 128))
+        act(a("wa"), ind(a("wv"), a("wl", 8, 16)))
         reg("p", [mm(bank(5, 300, 428), a("wa"), IN, True, True)])
-        act(a("nb"), bank(1, 136, 144), scale=-262144.0, bias=67108864.0)
-        act(a("wt"), bank(5, 300, 428))
-        if rnd == 1:
-            old_mm()
-        yc = [a("yc", 512 * b, 512 * b + 512) for b in range(4)]
-        src = [ind(a("mu"), a("cu", 32 * b, 32 * b + 32)) for b in range(4)]
+        if rnd == 0:
+            act(a("nb"), bank(7, 0, 8), scale=-262144.0, bias=67108864.0)
+        else:
+            act(a("nb"), bank(7, 0, 8), bias=-256.0)
+        act(a("wt"), bank(5, 300, 428), scale=SG)
+        if rnd == 0:
+            reg("p", [mm(bank(6, 16, 24), I16, CW, False, False), mm(bank(6, 16, 24), I16, SV, False, False), mm(bank(6, 24, 32), I1, SV, False, False)])
+        else:
+            reg("p", [mm(bank(6, 0, 8), I1, SV, False, False)])
+        reg("p", [mm(bank(7, 0, 128), I1, a("krow"), True, False)])
+        yc = [a("m1", YC + 512 * b, YC + 512 * b + 512) for b in range(4)]
+        ab = [a("m1", AB + 512 * b, AB + 512 * b + 512) for b in range(4)]
+        src = [ind(a("mu", 0, W), a("cu", 32 * b, 32 * b + 32)) for b in range(4)]
         act(yc[0], src[0])
         cp(yc[2], src[2])
         act(yc[1], src[1])
         cp(yc[3], src[3])
-        reg("p", [mm(bank(7, 0, 128), I1, a("krow"), True, False)])
-        for b in (2, 0, 3, 1):
-            reg("p", [mm(bank(b, 0, 512), a("wt"), a("ex", 512 * b, 512 * b + 512), True, False)])
-        for b in (2, 0, 3, 1):
-            reg("p", [mm(bank(b, 0, 512), I1, yc[b], False, True)])
-        reg("p", [mm(bank(7, k, 128, 16), a("yc", k, 2048, 16), a("gn"), False, False) for k in range(16)])
-        for b in range(2):
-            act(a("ab", 512 * b, 512 * b + 512), bank(b, 0, 512), F.Relu)
-            ts(a("ab", 1024 + 512 * b, 1536 + 512 * b), bank(2 + b, 0, 512), 0.0, A.max)
-        reg("p", [mm(bank(7, k, 128, 16), a("ab", k, 2048, 16), a("gp"), False, k == 15) for k in range(16)])
-        act(a("cf"), ind(a("rlw"), a("wl", 8, 16)))
-        ts(a("ll", 0, 13), bank(5, 256, 269), 1.0 / 16, A.mult, 7.0, A.add)
-        one = bank(1, 0, 128)
-        reg("p", [mm(one, a("k0"), I1, True, False)])
+        for b in (0, 2, 1, 3):
+            reg("p", [mm(bank(b, 0, 512), a("wt"), a("ex", 512 * b, 512 * b + 512), True, b >= 2)])
+            if b == 1:
+                reg("p", [mm(bank(0, 0, 512), I1, yc[0], False, True)])
+        reg("p", grp(bank(5, 0, 128), [(a("blk"), qr), (a("blk"), a("crow"))]))
+        reg("p", [mm(bank(1, 0, 512), I1, yc[1], False, True)])
+        reg("p", [mm(bank(7, k, 128, 16), a("m1", YC + k, YC + 2048, 16), a("gn"), False, False) for k in range(16)])
+        tt(ab[2], yc[2], bank(2, 0, 512), A.max)
+        act(ab[0], bank(0, 0, 512), F.Relu)
+        tt(ab[3], yc[3], bank(3, 0, 512), A.max)
+        act(ab[1], bank(1, 0, 512), F.Relu)
+        reg("p", [mm(bank(7, k, 128, 16), a("m1", AB + k, AB + 2048, 16), a("gp"), False, k == 15) for k in range(16)])
+        (cp, act)[rnd](a("cf"), ind(a("rlw"), a("wl", 0, 8)))
+        one, P1, P2 = bank(0, 0, 128), bank(2, 0, 128), bank(3, 0, 128)
         if rnd == 0:
-            slot_rows()
-            slot_mm()
-            old_mm()
-            act(a("junk", 1200, 1400), bank(4, 200, 400), acc=c1("thf", 2))
-        tt(a("oul", 0, 128), ind(a("upp"), a("cl")), a("oh"), A.mult)
-        tt(a("oul", 136, 264), a("oh"), a("oul", 0, 128), A.subtract)
-        if rnd == 1:
-            slot_mm()
-            tt(a("same"), a("cr", 8, 272), a("cr", 7, 271), A.is_equal)
-        reg("s", [actv(a("dab", 128 * t, 128 * t + 128), bank(4, 0, 128), F.Abs, 262144.0, c1("nb", t)) for t in range(8)])
-        scan(a("km"), a("rsk"), bank(7, 0, 128), A.add, A.min)
-        scan(a("kn"), a("rsk"), bank(7, 0, 128), A.add, A.min)
-        tt(a("eq", 16, 144), ind(a("km"), a("lsu")), a("kn"), A.is_equal)
-        reg("p", grp(one, [(a("eq", 16, 144), I1), (a("eq", 15, 143), IN)], False))
-        tt(a("vm"), bank(5, 0, 128), a("cf"), A.subtract)
-        tt(a("pr"), one, a("cf"), A.mult)
-        reg("p", [mm(bank(6, 0, 128), a("blk32"), a("pr"), False, False), mm(bank(6, 136, 264), a("blk32"), a("pr"), False, True)])
-        tt(a("vm2"), bank(5, 128, 256), a("vm"), A.mult)
-        if rnd == 0:
-            tt(a("same"), a("cr", 8, 272), a("cr", 7, 271), A.is_equal)
+            wrap(bank(6, 16, 32), lambda r: qrow(3, 2, r), False)
+            reg("p", grp(P1, [(top("d1", 2), top("half", 2)), (a("s1b"), qr), (a("s1b"), a("crow"))], True, False))
+            reg("p", grp(P2, [(top("d2", 1), top("half", 1)), (a("s2b"), qr), (a("s2b"), a("crow"))], True, False))
         else:
-            cls[0]()
-        tt(a("val"), bank(6, 0, 264), a("oul"), A.mult)
-        if rnd == 1:
-            cls[1]()
-        tt(a("tr"), one, a("vm2"), A.mult)
-        if rnd == 1:
-            cls[2]()
-        scan(a("seg", 8, 272), a("same"), a("val"), A.mult, A.add)
+            wrap(bank(6, 0, 8), lambda r: qrow(2, 1, r), False, True, "cs2")
+            reg("p", grp(P2, [(a("s2b"), qr), (a("s2b"), a("crow"))], True, False))
+        HJ = a("hj") if rnd == 0 else bank(6, 8, 16)
+        rhyme = [lambda: scan(a("dmn"), a("rsj"), a("dab"), A.add, A.min),
+                 lambda HJ=HJ: tt(a("da"), HJ, a("dmn", 127, 1024, 128), A.subtract),
+                 lambda: tt(a("db"), a("da"), a("dump"), A.min),
+                 lambda: ts(a("dl"), a("db"), 256.0, A.add),
+                 lambda: scatter(a("rlw"), a("dl"), a("tr"), a("cf"))]
         if rnd == 0:
-            cp(c1("bi", 0), c1("thf", 2))
-            tt(a("zt", 0, 208), ind(a("seg", 0, 136), a("ll", 0, 13)), a("zt", 0, 208), A.add)
-            ts(c1("bi", 1), c1("bi", 0), 15, A.bitwise_and)
-            tt(a("zt", 256, 464), ind(a("seg", 136, 272), a("ll", 0, 13)), a("zt", 256, 464), A.add)
-            tt(c1("thf", 1), c1("bi", 1), c1("thf", 0), A.add)
-            reg("y", [(None, [], [a("xb", V, W)])], "a")
-            ghosts("xb")
+            reg("s", [actv(a("dab", 128 * t, 128 * t + 128), bank(4, 0, 128), F.Abs, 262144.0, c1("nb", t)) for t in range(8)])
+            tt(a("vm"), bank(5, 0, 128), a("cf"), A.subtract)
+            first(1, 0, 0, 24)
+            scan(a("km"), a("rsk"), bank(7, 0, 128), A.add, A.min)
+            cp(a("ks"), bank(7, 0, 128))
         else:
-            cls[3]()
-            tt(a("pt", 0, 208), ind(a("seg", 0, 136), a("ll", 0, 13)), a("pt", 0, 208), A.add)
-            dma("y", [(hbm(T.up1[:], "out1"), a("pt", 0, 200))])
-            cls[4]()
+            for t in range(8):
+                ts(a("dab", 128 * t, 128 * t + 128), a("jq"), c1("nb", t), A.not_equal, 262144.0, A.mult)
+            act(a("ks"), bank(7, 0, 128))
+            rhyme[0]()
+            scan(a("km"), a("rsk"), bank(7, 0, 128), A.add, A.min)
+            tt(a("vm"), bank(5, 0, 128), a("cf"), A.subtract)
+        tt(a("eq"), ind(a("km"), a("lsu")), a("ks"), A.is_equal)
+        reg("p", [mm(one, a("eq"), I1, True, True)])
+        if rnd == 0:
+            cp(a("sl", 16, 32), bank(6, 16, 32))
+        else:
+            rhyme[1]()
+            cp(a("sl", 0, 8), bank(6, 0, 8))
+            rhyme[2]()
+        tt(a("tr"), one, a("vm"), A.mult)
+        if rnd == 0:
+            reg("p", [mm(P1, a("l1m"), a("tr"), False, True)])
+        reg("p", [mm(P2, a("l2m"), a("tr"), False, True)])
+        if rnd == 0:
+            act(a("xv"), ind(a("xa"), a("wl", 8, 16)))
+            first(1, 0, 24, 40)
+            ts(a("rr"), P1, MR, A.add, MR2, A.subtract)
+            tt(a("val"), P2, a("rr"), A.add)
+            scatter(a("wb"), a("sl", 24, 32), a("val"))
+            for nms in ((0, 1), (2,)):
+                for tb in (0, 1):
+                    dma("y", [(tab(("ft", "rt", "ht")[j], tb), wrow(j, tb)) for j in nms])
+            act(a("vb"), a("val"), scale=MK)
+            wrap(bank(1, 0, 8), lambda r: a("vb", r, 128, 16))
+            act(a("junk", 1248, 1448), bank(4, 200, 400), acc=c1("thf", 2))
+            act(c1("thf", 3), c1("thf", 2), bias=-7.5)
+            act(c1("thf", 4), c1("thf", 2), bias=c1("thf", 0))
+            act(c1("thf", 5), c1("thf", 3), bias=M16)
+            act(c1("thf", 6), c1("thf", 5), bias=-M16)
+            act(c1("thf", 1), c1("thf", 6), scale=-1.0, bias=c1("thf", 4))
+            ghosts("xb", ("m1", 0), ("m1", ML), ("mu", 0))
+            act(a("hj"), bank(6, 8, 16))
+            first(1, 0, 40, 144)
+            ts(a("cc"), bank(1, 0, 8), -8.5, A.add)
+            place_mm(0)
+            tt(a("pv"), ind(a("xb"), a("cc")), a("xv"), A.max)
+            place(0)
+            first(1, 0, 144, 200)
+            place_mm(1)
+            for tb in (1, 0):
+                reg("p", grp(bank(4 + tb, 0, 200), [(I1, tab("ft", tb, 200)), (I1, tab("rt", tb, 200))]))
+            ts(a("l1", 200, 400), bank(5, 0, 200), -8.5, A.add)
+            scatter(a("m1", 0, LO + V), a("sl", 16, 24), a("pv"))
+            again(0, 0, 64)
+            again(0, 64, 200)
+            place(1)
+            first(1, 1, 0, 120, 0)
+            first(1, 1, 120, 200, 120)
+        else:
+            act(a("val"), P2)
+            rhyme[3]()
+            rhyme[4]()
             dma("y", [(hbm(T.rl1[:], "out3"), a("rlw", 0, 512))])
-            tt(a("pt", 256, 464), ind(a("seg", 136, 272), a("ll", 0, 13)), a("pt", 256, 464), A.add)
-            dma("s", [(hbm(T.lo1[:], "out2"), a("pt", 256, 456))])
+            scatter(a("ow"), a("sl", 0, 8), a("val"))
+            dma("s", [(hbm(T.up1[:], "out1"), owrows(0)), (hbm(T.lo1[:], "out2"), owrows(1))])
     reg("y", [(None, [hbm(None, "out%d" % i) for i in range(4)], [])], "n")
     reg("g", [(None, [], [])], "e")
 
@@ -444,12 +573,12 @@ def rank_program(g, core, T, topo):
     for i, o in enumerate(ops):
         e = o["e"]
         use = [(r, False) for r in o["r"]] + [(r, True) for r in o["w"]]
-        use = [((nm, lo // 512 * 512, -(-hi // 512) * 512), wr) if nm == "ps" else ((nm, lo, hi), wr) for (nm, lo, hi), wr in use]
+        use = [((nm, lo // 512 * 512, -(-hi // 512) * 512, pm), wr) if nm == "ps" else ((nm, lo, hi, pm), wr) for (nm, lo, hi, pm), wr in use]
         need = {}
-        for (nm, lo, hi), wr in use:
-            for l2, h2, w2, j in hist.get(nm, []):
+        for (nm, lo, hi, pm), wr in use:
+            for l2, h2, p2, w2, j in hist.get(nm, []):
                 src = ops[j]["src"]
-                if l2 < hi and lo < h2 and ((src != e) if nm == "ps" else (wr or w2)) and not (src == "p" and e == "p"):
+                if l2 < hi and lo < h2 and pm & p2 and ((src != e) if nm == "ps" else (wr or w2)) and not (src == "p" and e == "p"):
                     need[src] = max(need.get(src, -1), j)
         o["waits"] = []
         for src, j in sorted(need.items(), key=lambda t: -t[1]):
@@ -460,8 +589,8 @@ def rank_program(g, core, T, topo):
                     know[e][s2] = max(know[e].get(s2, -1), j2)
         o["src"] = e if o["k"] == "c" else "z%d" % i
         o["know"] = dict(know[e]) if o["k"] != "a" else {}
-        for (nm, lo, hi), wr in use:
-            hist.setdefault(nm, []).append((lo, hi, wr, i))
+        for (nm, lo, hi, pm), wr in use:
+            hist.setdefault(nm, []).append((lo, hi, pm, wr, i))
     count = {e: 0 for e in queue}
     nd = 0
     for o in ops:

@@ -2,19 +2,17 @@ from concourse.bass import DstId, RemoteDMATransfer
 from concourse.mybir import AluOpType, AxisListType, ActivationFunctionType
 
 V, W, NR = 3200, 4096, 8
-RS = 272
-LO = 16 * RS
+LO = 4352
 SPEC = {
-    "bfloat16": "xa 4096 xb 4096 wv 3328 m1 12800 mu 7552 wb 8704 qb 6400 ad 6400 ft 544 rt 544 ht 544 sb 1792 nrow 208 krow 128 jq 128 "
-                "id1 128 idn 128 idk 128 i16 128 ones 128 half 128 blk 128 mt 128 s1b 128 s2b 128 d1 128 d2 128 cs 144 cs2 144 g1 8 gp 8 gn 8 "
-                "ca 200 cb 200 cd 200 c160 208 cw 16 ee 32 sv 16 rsk 128 rsj 1024 bad 208 low 208 sc 208 junk 1456 cmp 432 oh 128 wa 128 wt 128 "
-                "xv 128 pv 128 crow 128 ex 2048 dab 1024 dmn 1024 eq 128 lw 128 vb 128 hs 208",
-    "float32": "zt 544 pt 472 c16 72 rlw 640 thf 8 col 24 jp 128 t16 8 jc 8 jh 8 dump 8 l1m 128 l2m 128 ow 9480 tu 200 duc 200 kt 208 tm 200 "
-               "acc 8 cf 128 vm 128 tr 128 nb 8 hj 8 da 8 db 8 km 128 ks 128 rr 128 val 128",
-    "int32": "ti 400 rli 512 sni 56 thi 4 lsi 8",
-    "uint16": "l1 400 lp 472 l2 400 snu 56 lsu 8 cl 8 wl 16 sl 32 cu 128 dl 8 cc 8",
+    "bfloat16": "xa 4096 xb 4096 wv 3328 m1 12800 m2 8192 mu 7552 yy 4096 ad 6400 ht 400 sb 1792 nrow 208 krow 128 jq 128 id1 128 idn 128 "
+                "dm 128 jc 8 nc 8 i16 128 ones 128 blk 128 mt 128 cs 144 cs2 144 g1 8 gp 8 gn 8 ca 200 cd 200 c160 208 cw 16 ee 24 sv 24 rsk 128 rsj 1024 bad 208 low 208 "
+                "sc 208 junk 1456 cmp 432 oh 128 wa 128 wt 128 xv 128 pv 128 crow 128 ex 2048 dab 1024 dmn 1024 eq 128 lw 128 hs 208",
+    "float32": "pt 400 rlw 640 thf 8 col 16 jp 128 t16 8 jh 8 dump 8 id32 128 in32 128 nb32 128 g32 8 cm 128 ow 10632 tu 200 duc 200 kt 208 "
+               "tm 200 acc 8 cf 128 vm 128 tr 128 nb 8 hj 8 da 8 db 8 km 128 ks 128 val 128",
+    "int32": "ti 400 rli 512 sni 56 thi 4",
+    "uint16": "l1 400 ln 400 snu 56 lsu 8 cl 8 wl 16 sl 16 cu 128 dl 8 cc 8",
 }
-SCRATCH = {"ps": ("psum", [128, 4096], "float32"), "qq": ("sbuf", [128, 5, 128], "bfloat16")}
+SCRATCH = {"ps": ("psum", [128, 4096], "float32"), "qq": ("sbuf", [128, 4, 128], "bfloat16")}
 for _d, _s in SPEC.items():
     _w = _s.split()
     for _i in range(0, len(_w), 2):
@@ -23,8 +21,11 @@ SEMAPHORES = ["ev", "es", "ep", "eg", "arr", "sent"] + ["d%d" % i for i in range
 
 SEC = [(0, 0, 64), (0, 64, 128), (0, 128, 200), (1, 0, 56), (1, 56, 120), (1, 120, 176), (1, 176, 200)]
 SLOT = [0, 1024, 2048, 3072, 4096, 5120, 6016, 6400]
+OFF = (156, 148)
+CUT, HOP = 120, (180, 172)
+SBS = 32
+REFILL, SUMS = {1: 3, 2: 4, 3: 5, 4: 6}, {1: 0, 3: 1, 4: 2, 5: 3, 6: 4}
 M16 = 1.5 * 2.0 ** 27
-M512 = 1.5 * 2.0 ** 32
 HB = 66048
 BIG = 1 << 23
 ALL = 0xFFFF
@@ -48,9 +49,6 @@ def rank_program(g, core, T, topo):
     def part(name, j, lo, hi):
         return (T[name][j:128:16, lo:hi], [(name, lo, hi, 1 << j)])
 
-    def top(name, n):
-        return (T[name][0:n, :], a(name)[1])
-
     def c1(name, i):
         return a(name, i, i + 1)
 
@@ -60,9 +58,9 @@ def rank_program(g, core, T, topo):
     def bank(b, lo, hi, st=1):
         return a("ps", 512 * b + lo, 512 * b + hi, st)
 
-    def qrow(i, n=1, r=None):
-        ap = T.qq[:, i, :] if r is None else T.qq[:, i:i + n, r:128:16]
-        return (ap, [("qq", 128 * i, 128 * (i + n), ALL)])
+    def qrow(i, n=1, r=None, st=1):
+        ap = T.qq[:, i, :] if r is None else T.qq[:, i:i + n:st, r:128:16]
+        return (ap, [("qq", 128 * j, 128 * j + 128, ALL) for j in range(i, i + n, st)])
 
     def ind(w_, o):
         return (w_[0].indirect(o[0]), w_[1] + o[1])
@@ -86,8 +84,11 @@ def rank_program(g, core, T, topo):
     def tt(o, i, j, op):
         reg("v", [(lambda: ve.tensor_tensor(o[0], i[0], j[0], op), [i, j], [o])])
 
+    def cpv(o, i):
+        return (lambda: ve.tensor_copy(o[0], i[0]), [i], [o])
+
     def cp(o, i):
-        reg("v", [(lambda: ve.tensor_copy(o[0], i[0]), [i], [o])])
+        reg("v", [cpv(o, i)])
 
     def scatter(w_, o, i, j=None):
         out = w_[0].indirect(o[0])
@@ -102,8 +103,8 @@ def rank_program(g, core, T, topo):
     def red(o, i):
         reg("v", [(lambda: ve.tensor_reduce(o[0], i[0], AxisListType.X, A.add), [i], [o])])
 
-    def zero(o):
-        reg("v", [(lambda: ve.memset(o[0], 0.0), [], [o])])
+    def mset(o, c):
+        reg("v", [(lambda: ve.memset(o[0], c), [], [o])])
 
     def actv(o, i, f=F.Identity, scale=1.0, bias=0.0, acc=None):
         if acc is None:
@@ -122,11 +123,8 @@ def rank_program(g, core, T, topo):
     def wrap(o, src, s0=True, s1=True, by="cs"):
         reg("p", grp(o, [(a(by, 15 - r, 143 - r), src(r)) for r in range(16)], s0, s1))
 
-    def iota(o, pat, base=0, cm=0, whole=False):
-        if whole:
-            reg("g", [(lambda: g.iota(o[0], pat, base, cm), [], [o])])
-        else:
-            reg("g", [(lambda: g.iota(o[0], pat, base, cm, allow_small_or_imprecise_dtypes=True), [], [o])])
+    def iota(o, pat, base=0, cm=0):
+        reg("g", [(lambda: g.iota(o[0], pat, base, cm, allow_small_or_imprecise_dtypes=True), [], [o])])
 
     def fill(o, n, v):
         iota(o, [[0, n]], v)
@@ -137,154 +135,111 @@ def rank_program(g, core, T, topo):
     def dma(e, pairs):
         reg(e, [((o[0], i[0]), [i], [o]) for o, i in pairs], "d")
 
-    PF, RC, R85, MK, MR, MR2, RRS, UP, UPB, UP256, SG = [c1("col", i) for i in range(11)]
-    tmp = [c1("col", i) for i in range(12, 20)]
+    PF, RC, UP, DOWN, SG = [c1("col", i) for i in range(5)]
+    tmp = [c1("col", i) for i in range(8, 12)]
     I1, IN, I16 = a("id1"), a("idn"), a("i16")
-    qo, qh, qr, ql, qp = [qrow(i) for i in range(5)]
+    qh, ql, qr, qm = [qrow(i) for i in range(4)]
     nr = a("nrow", 0, 128)
 
-    def tab(nm, tb, n=RS):
-        return a(nm, RS * tb, RS * tb + n)
-
-    def wrow(j, tb):
-        return part("wb", j, LO * tb, LO * tb + LO)
+    def tab(nm, tb, lo=0, hi=200):
+        return a(nm, 200 * tb + lo, 200 * tb + hi)
 
     def owrows(tb):
-        return part("ow", FULL, V * tb, V * tb + V)
-
-    dma("y", [(a("ti", 0, 200), hbm(T.up[:])), (a("ti", 200, 400), hbm(T.lo[:]))])
-    dma("y", [(a("xa"), hbm(T.x[:]))])
-    iota(PF, [[0, 1]], 0, 1)
-    iota(a("nrow"), [[1, 208]])
-    iota(a("c16"), [[16, RS - 200]], V)
-    iota(a("t16"), [[16, 8]])
-    zero(a("wb", 0, LO // 2))
-    zero(a("wb", LO // 2, LO))
-    act(tmp[0], PF, bias=-7.5)
-    act(tmp[1], tmp[0], bias=M16)
-    act(tmp[2], tmp[1], bias=-M16)
-    act(RC, tmp[2], scale=-1.0, bias=PF)
-    act(R85, RC, bias=8.5)
-    act(a("zt", 200, RS), a("c16"), bias=R85)
-    act(a("zt", RS + 200, 2 * RS), a("c16"), bias=R85)
-    act(a("wb", LO, LO + LO // 2), a("wb", 0, LO // 2))
-    act(tmp[3], RC, F.Sign, -1.0, 1.5)
-    act(tmp[4], RC, F.Sign, -1.0, 7.5)
-    act(tmp[5], RC, F.Relu, 1.0, -1.0)
-    act(MK, tmp[3], F.Relu)
-    ts(IN, nr, PF, A.is_equal, -1.0, A.mult)
-    ts(I1, nr, PF, A.is_equal)
-    ts(a("idk"), nr, PF, A.is_equal, float(LO), A.mult)
-    fill(a("wb", LO + LO // 2, 2 * LO), LO // 2, 0)
-    fill(a("cs"), 144, 0)
-    fill(a("ones"), 128, 1)
-    glo, ghi = ([[-16, 8]], A.is_ge, 0.0, 0, 1), ([[16, 8]], A.is_ge, 0.0, 15, -1)
-    blo, bhi = ([[-16, 8], [0, 16]], A.is_ge, 0.0, 0, 1), ([[16, 8], [0, 16]], A.is_ge, 0.0, 15, -1)
-    diag = [[-1, 128]]
-    sel(a("g1"), a("ones", 0, 8), *glo)
-    sel(a("cs", 15, 128, 16), a("g1"), *ghi)
-
-    def parts(tb):
-        ts(tab("zt", tb, 200), a("ti", 200 * tb, 200 * tb + 200), 8.5, A.add)
-        ts(tab("ft", tb), tab("zt", tb), M16, A.add, M16 + 16.0, A.subtract)
-        reg("p", [mm(bank(5 - tb, 0, RS), IN, tab("ft", tb), True, True)])
-        if tb == 0:
-            cp(a("l1"), a("ti"))
-        tt(tab("rt", tb), bank(5 - tb, 0, RS), tab("zt", tb), A.add)
-        dma("y", [(wrow(0, tb), tab("ft", tb)), (wrow(1, tb), tab("rt", tb))])
-
-    def place_mm(tb):
-        reg("p", grp(bank(3 - tb, 0, 200), [(I1, tab("ft", tb, 200)), (a("idk"), tab("rt", tb, 200))]))
-
-    def place(tb):
-        ts(tab("lp", tb, 200), bank(3 - tb, 0, 200), 1.0 / 16, A.mult, -8.5 * RS, A.add)
+        return part("ow", FULL, LO * tb, LO * tb + V)
 
     def classes():
-        fu, fl, ru, rl_, hu, hl = [tab(nm, tb, 200) for nm in ("ft", "rt", "ht") for tb in (0, 1)]
-        reg("p", grp(bank(7, 256, 456), [(I1, fl), (I1, rl_), (I1, hu), (IN, hl), (IN, fu), (IN, ru)])
-            + grp(bank(6, 256, 456), [(I1, fu), (I1, ru), (I1, a("ca")), (I1, a("cb")), (I1, a("cd")), (IN, hu)]))
-
-    act(UP, tmp[4], F.Relu)
-    act(UPB, tmp[4], scale=-256.0)
-    act(MR, tmp[5], scale=M512 - M16, bias=M16)
-    act(MR2, tmp[5], scale=M512 - M16 - HB, bias=M16)
-    act(UP256, UP, scale=256.0)
-    act(RRS, RC, scale=float(RS))
-    act(SG, PF, F.Sign, -1.0, 63.5)
-    act(a("jc"), a("t16"), bias=RC)
-    act(a("jh"), a("jc"), bias=0.5)
-    act(a("ee", 8, 16), a("jc"), scale=1024.0, bias=-127 * 1024.0)
-    act(a("dump"), a("jc"), bias=256.0)
-    act(I16, I1, scale=16.0)
-    parts(0)
-    place_mm(0)
-    place(0)
-    parts(1)
-    place_mm(1)
-    place(1)
-    dma("y", [(a("xb", 1536, V), hbm(T.x[:, 1536:V]))])
-    act(a("cb"), a("ft", 0, 200), scale=0.0, bias=-8.5)
-    act(a("xb", 0, 512), a("xa", 0, 512))
-    act(a("ht"), a("ft"), bias=65800.0)
-    act(a("xb", 512, 1536), a("xa", 512, 1536))
+        reg("p", grp(bank(7, 256, 456), [(a("id32"), tab("pt", 1)), (a("in32"), tab("pt", 0)), (I1, tab("ht", 0)), (IN, tab("ht", 1))])
+            + grp(bank(6, 256, 456), [(a("id32"), tab("pt", 0)), (IN, tab("ht", 0)), (I1, a("ca")), (I1, a("cd"))]))
 
     def ghosts(src, *to):
         for nm, o in to:
             sel(a(nm, o + V, o + W), a(src, V, W), [[0, W - V]], A.is_ge, 0.0, 0, 0)
 
-    def spread(b):
-        sel(a("ex", 512 * b, 512 * b + 512), a("ex", 512, 1024), [[-1, 32], [0, 16]], A.is_equal, 0.0, -32 * b, 1)
+    WINDOWS = (("m1", 0), ("m2", 0), ("m1", ML), ("m2", W), ("yy", 0))
 
-    fill(a("ca"), 200, -256)
-    fill(a("cd"), 200, HB)
-    classes()
-    ghosts("xa", ("m1", 0), ("m1", ML))
-    for nm, n, v in (("mt", 128, -1), ("rsk", 128, 0), ("c160", 208, 160)):
+    dma("y", [(tab("ti", 0), hbm(T.up[:])), (tab("ti", 1), hbm(T.lo[:]))])
+    dma("y", [(a("xa", 0, 2048), hbm(T.x[:, 0:2048]))])
+    dma("y", [(a("xa", 2048, W), hbm(T.x[:, 2048:W]))])
+    dma("y", [(a("xb", 2048, V), hbm(T.x[:, 2048:V]))])
+    dma("y", [(a("wv", 0, V), hbm(T.w[:]))])
+    glo, ghi = ([[-16, 8]], A.is_ge, 0.0, 0, 1), ([[16, 8]], A.is_ge, 0.0, 15, -1)
+    blo, bhi = ([[-16, 8], [0, 16]], A.is_ge, 0.0, 0, 1), ([[16, 8], [0, 16]], A.is_ge, 0.0, 15, -1)
+    diag = [[-1, 128]]
+    iota(PF, [[0, 1]], 0, 1)
+    iota(a("nrow"), [[1, 208]])
+    iota(a("t16"), [[16, 8]])
+    for nm, n, v in (("ones", 128, 1), ("cs", 144, 0), ("mt", 128, -1)):
         fill(a(nm), n, v)
-    fill(a("wv", V, V + 128), 128, 0)
+    sel(a("g1"), a("ones", 0, 8), *glo)
     sel(a("blk"), a("ones"), *blo)
-    sel(a("mt"), a("mt"), *bhi)
+    sel(a("cs", 15, 128, 16), a("g1"), *ghi)
     sel(a("blk"), a("blk"), *bhi)
+    sel(a("mt"), a("mt"), *bhi)
+    fill(a("ca"), 200, -256)
     sel(a("mt"), a("mt"), diag, A.is_gt, 0.0, 0, 1)
-    iota(a("krow"), [[0, 8], [1, 16]])
+    fill(a("cd"), 200, HB)
     sel(a("mt"), a("mt"), diag, A.not_equal, 256.0, 0, 1)
+    iota(a("krow"), [[0, 8], [1, 16]])
     iota(a("jp"), [[1, 128]], 257)
-    iota(a("lsi"), [[16, 8]], 15, 0, True)
-    fill(a("rsk", 0, 128, 16), 8, BIG)
-    for nm, lo, v in (("cw", 0, 256), ("cw", 8, 0), ("ee", 16, 0), ("bad", 200, 1), ("low", 200, 0), ("hs", 200, 256), ("cmp", 208, -26), ("cmp", 424, -26)):
-        fill(a(nm, lo, lo + 8), 8, v)
-    fill(a("rlw", 512, 640), 128, 0)
-    iota(a("s1b"), [[0, 64], [-2, 2]], 1)
-    iota(a("s2b"), [[0, 64], [1, 2]])
-    for side in (blo, bhi):
-        sel(a("s1b"), a("s1b"), *side)
-        sel(a("s2b"), a("s2b"), *side)
-    iota(a("d1"), [[0, 32], [-248, 2], [15, 2]], -8, 1)
-    iota(a("d2"), [[0, 64], [17, 2]])
-    ghosts("xa", ("mu", 0))
-    fill(a("ex", 512, 1024), 512, 1)
-    spread(2)
-    spread(0)
+    ghosts("xa", *WINDOWS)
+    for nm, lo, n, v in (("c160", 0, 208, 160), ("wv", V, 128, 0), ("rlw", 512, 128, 0), ("m1", W, LO - W, 0), ("cw", 0, 8, 256), ("cw", 8, 8, 0),
+                         ("ee", 16, 8, 0), ("bad", 200, 8, 1), ("low", 200, 8, 0), ("hs", 200, 8, 256), ("cmp", 208, 8, -26), ("cmp", 424, 8, -26)):
+        fill(a(nm, lo, lo + n), n, v)
+    for nm, v, st in (("rsj", -1024.0, 128), ("rsk", 0.0, 16)):
+        mset(a(nm), v)
+        mset(a(nm, 0, None, st), float(BIG))
+    ts(IN, nr, PF, A.is_equal, -1.0, A.mult)
+    ts(I1, nr, PF, A.is_equal)
+    ts(a("lsu"), a("t16"), 15.0, A.add)
+    reg("v", [cpv(a("ex", k, 2048, 16), I1) for k in range(16)])
+    cp(a("l1"), a("ti"))
+    cp(a("pt"), a("ti"))
+    cp(a("xb", 0, 2048), a("xa", 0, 2048))
+    act(tmp[0], PF, bias=-7.5)
+    act(tmp[1], tmp[0], bias=M16)
+    act(tmp[2], tmp[1], bias=-M16)
+    act(RC, tmp[2], scale=-1.0, bias=PF)
+    act(SG, PF, F.Sign, -1.0, 63.5)
+    act(tmp[3], RC, F.Sign, -1.0, 7.5)
+    act(a("jc"), a("t16"), bias=RC)
+    act(UP, tmp[3], F.Relu)
+    act(DOWN, tmp[3], F.Relu, -1.0)
+    act(a("jh"), a("jc"), bias=0.5)
+    act(a("ee", 0, 8), a("jc"), scale=1024.0, bias=-127 * 1024.0)
+    act(a("dump"), a("jc"), bias=256.0)
+    for nm, src, sc in (("i16", I1, 16.0), ("id32", I1, 1.0), ("in32", I1, -1.0), ("gn", a("cs", 15, 128, 16), -16.0), ("gp", a("cs", 15, 128, 16), 32.0),
+                        ("cs2", a("cs"), 200.0), ("g32", a("cs", 15, 128, 16), 1.0), ("nb32", a("blk"), -1.0)):
+        act(a(nm), src, scale=sc)
+    act(a("ht"), a("pt"), bias=65792.5)
+    classes()
 
     def first(rnd, tb, lo, hi, cut=None):
         xn, xo = ("xa", "xb") if rnd == 0 else ("xb", "xa")
-        tt(a("m1", ML * tb + 16 * lo, ML * tb + 16 * hi), ind(a(xn), a("l1", 200 * tb + lo, 200 * tb + hi)), a(xo, 16 * lo, 16 * hi), A.max)
+        tt(a("m1", ML * tb + 16 * lo, ML * tb + 16 * hi), ind(a(xn), tab(("l1", "ln")[rnd * tb], tb, lo, hi)), a(xo, 16 * lo, 16 * hi), A.max)
         if cut is not None:
             again(tb, cut, hi)
 
     def again(tb, lo, hi):
         dma("y", [(a("mu", LO * tb + 16 * lo, LO * tb + 16 * hi), a("m1", ML * tb + 16 * lo, ML * tb + 16 * hi))])
 
-    def twice(tb, hf):
-        o = V * tb + 1600 * hf
-        act(a("qb", o, o + 1600), ind(a("wb", LO * tb, LO * tb + LO), a("lp", RS * tb + 100 * hf, RS * tb + 100 * hf + 100)), scale=MK)
+    def aside(rnd, step):
+        c0, h = 16 * OFF[rnd], 8 * (200 - OFF[rnd])
+        G, R = [[a("ad", o + h * j, o + h * j + h) for j in (0, 1)] for o in (0, 1024)]
+        D, S = [[bank(b + j, 0, h) for j in (0, 1)] for b in (4, 2)]
+        if step == 0:
+            act(a("ad", 0, 2 * h), ind(a(("xa", "xb")[rnd]), tab("l1", 0, OFF[rnd], 200)))
+            for j in (0, 1):
+                reg("p", grp(D[j], [(I1, a("xa", c0 + h * j, c0 + h * j + h)), (IN, G[j])]))
+            reg("p", [mm(S[j], I1, G[j], True, False) for j in (0, 1)])
+        for j in (0, 1):
+            if step == 1:
+                act(R[j], D[j], F.Relu)
+                reg("p", [mm(S[j], I1, R[j], False, True)])
+            elif step == 2:
+                act(a("m1", c0 + h * j, c0 + h * j + h), S[j])
 
-    def twice_mm(tb, hf):
-        o = V * tb + 1600 * hf
-        wrap(bank(7 - tb, 100 * hf, 100 * hf + 100), lambda r: a("qb", o + r, o + 1600, 16))
-
-    def qlist(tb):
-        ts(a("l2", 200 * tb, 200 * tb + 200), bank(7 - tb, 0, 200), -8.5, A.add)
+    def hop(rnd, tb, lo, hi, by=act):
+        by(a("m2", W * tb + 16 * lo, W * tb + 16 * hi), ind(a("m1", ML * tb, ML * tb + W), tab(("l1", "ln")[rnd], tb, lo, hi)))
 
     def cuts(i):
         out, x = [], SLOT[i]
@@ -297,10 +252,10 @@ def rank_program(g, core, T, topo):
     def minus_w(i):
         reg("p", [mm(a("ps", o, o + n), IN, a("wv", x % V, x % V + n), o % 512 == 0, False) for o, x, n in cuts(i)])
 
-    def second(i):
+    def second(rnd, i):
         tb, lo, hi = SEC[i]
         o = a("mu", LO * tb + 16 * lo, LO * tb + 16 * hi)
-        tt(o, ind(a("m1", ML * tb, ML * tb + W), a("l2", 200 * tb + lo, 200 * tb + hi)), o, A.max)
+        tt(o, ind(a("m2", W * tb, W * tb + W), tab(("l1", "ln")[rnd], tb, lo, hi)), o, A.max)
 
     def plus_m(i):
         cs_ = cuts(i)
@@ -311,81 +266,60 @@ def rank_program(g, core, T, topo):
         act(a("ad", SLOT[i], SLOT[i + 1]), a("ps", 1024 * (i % 3), 1024 * (i % 3) + SLOT[i + 1] - SLOT[i]), F.Abs)
 
     def dist(i):
-        tb, lo, hi = SEC[i]
+        tb, lo, hi = SEC[i] if i < 5 else (1, SEC[5][1], 200)
         wrap(bank(7 - tb, lo, hi), lambda r: a("ad", V * tb + 16 * lo + r, V * tb + 16 * hi, 16))
 
-    def halves(lo, hi):
-        dma("y", [(part("mu", j, lo, hi), part("mu", j, LO + lo, LO + hi)) for j in range(8, 16)])
+    def halves(tb, lo, hi):
+        dma("y", [(part("yy", j, lo, hi), part("mu", j, LO * tb + lo, LO * tb + hi)) for j in range(8 * tb, 8 * tb + 8)])
 
-    first(0, 0, 0, 32)
-    first(0, 1, 0, 32)
-    dma("y", [(a("wv", 0, V), hbm(T.w[:]))])
-    first(0, 0, 32, 96, 0)
-    first(0, 1, 32, 96)
-    first(0, 0, 96, 200, 96)
+    first(0, 0, 0, 128, 0)
+    for step in range(3):
+        aside(0, step)
+    first(0, 0, 128, OFF[0])
+    again(0, 128, 200)
+    first(0, 1, 0, 120, 0)
     dma("y", [(c1("thi", 0), hbm(T.th[:])), (a("sni"), hbm(T.snd[:]))])
-    first(0, 1, 96, 200, 0)
+    first(0, 1, 120, 200, 120)
+    dma("y", [(a("rli"), hbm(T.rl[:]))] + [(owrows(tb), tab("pt", tb)) for tb in (0, 1)])
 
     for rnd in range(2):
-        for tb, hf in ((0, 0), (0, 1), (1, 0), (1, 1)):
-            twice(tb, hf)
-            if rnd == 1 and (tb, hf) == (0, 0):
-                for t2 in (0, 1):
-                    act(tab("pt", t2, 200), bank(4 + t2, 0, 200), bias=-8.5)
-                dma("y", [(owrows(t2), tab("pt", t2, 200)) for t2 in (0, 1)])
-        twice_mm(0, 0)
-        if rnd == 1:
-            classes()
-        twice_mm(0, 1)
-        qlist(0)
-        if rnd == 0:
-            dma("y", [(a("rli"), hbm(T.rl[:]))])
-            dma("y", [(wrow(2, tb), tab("ht", tb)) for tb in (0, 1)])
-            twice_mm(1, 0)
+        hop(rnd, 0, 0, 200)
+        hop(rnd, 1, 0, CUT)
         for i in range(3):
             minus_w(i)
         if rnd == 1:
-            twice_mm(1, 0)
+            classes()
         for i in range(7):
+            if (rnd, i) == (0, 4):
+                cp(a("snu"), a("sni"))
+                act(a("sb", 896, 896 + 16 * SBS), ind(a("mu", 0, V), a("snu", 0, SBS)), scale=UP)
+            if (rnd, i) == (0, 5):
+                cp(c1("thf", 0), c1("thi", 0))
             if i == 3:
-                qlist(1)
-                if rnd == 0:
-                    cp(c1("thf", 0), c1("thi", 0))
-                    cp(a("snu"), a("sni"))
-                    act(a("sb", 896, 1792), ind(a("mu", 0, V), a("snu")), scale=UP, bias=UPB)
-            second(i)
+                hop(rnd, 1, HOP[rnd], 200, cp)
+            second(rnd, i)
             plus_m(i)
-            if i == 0:
-                twice_mm(1, 1)
-            if 0 < i < 5:
-                minus_w(i + 2)
-            for j in {1: [0], 2: [1], 4: [2], 5: [3], 6: [4, 5]}.get(i, []):
-                dist(j)
             absd(i)
+            if i == 0:
+                hop(rnd, 1, CUT, HOP[rnd])
+            if i in REFILL:
+                minus_w(REFILL[i])
+            if i in SUMS:
+                dist(SUMS[i])
             if i == 6:
                 act(a("tu"), bank(7, 0, 200), scale=-1.0, bias=c1("thf", rnd))
                 act(a("duc"), bank(7, 0, 200))
-            if i >= 5:
-                halves(*((0, 16 * SEC[6][1]), (16 * SEC[6][1], V))[i - 5])
-        dist(6)
+            if i in (2, 6):
+                halves(i // 6, 0, V)
+        dist(5)
         if rnd == 0:
-            tt(a("sb", 896, 1792), ind(a("mu", LO, LO + V), a("snu")), a("sb", 896, 1792), A.min)
-            ts(a("sb", 0, 896), a("sb", 896, 1792), UP256, A.add)
-            reg("g", [(None, [a("sb", 0, 896)], [])], "x")
-            spread(3)
-            spread(1)
-            fill(a("m1", W, LO), LO - W, 0)
-            fill(a("rsj"), 1024, -1024)
-            fill(a("rsj", 0, 1024, 128), 8, BIG)
+            ts(a("sb", 0, 896), ind(a("mu", LO, LO + V), a("snu")), DOWN, A.mult)
+            ts(a("sb", 896 + 16 * SBS, 1792), ind(a("mu", 0, V), a("snu", SBS, 56)), UP, A.mult)
+            reg("g", [(None, [a("sb")], [])], "x")
+            ts(a("dm"), a("krow"), RC, A.is_equal)
             reg("y", [(None, [], [a("xb", V, W)])], "a")
-            act(a("gn"), a("cs", 15, 128, 16), scale=-16.0)
-            act(a("gp"), a("cs", 15, 128, 16), scale=32.0)
-            act(a("l1m"), a("s1b"), scale=-1.0)
-            act(a("l2m"), a("s2b"), scale=-1.0)
-            act(a("half"), a("ones"), scale=0.5)
         else:
-            dma("y", [(hbm(T.y[:], "out0"), a("mu", 0, V))])
-            act(a("cs2"), a("cs"), scale=200.0)
+            dma("y", [(hbm(T.y[:], "out0"), a("yy", 0, V))])
             for f in rhyme:
                 f()
 
@@ -404,10 +338,8 @@ def rank_program(g, core, T, topo):
         red(c1("acc", 6), a("cmp", 0, 216))
         red(c1("acc", 7), a("cmp", 216, 432))
         tt(a("hs", 0, 200), bank(6, 256, 456), a("tm"), A.add)
-        if rnd == 0:
-            cp(a("lsu"), a("lsi"))
         reg("p", [mm(bank(7, 0, 16), I1, a("cw"), True, False)])
-        CW = a("ee", 24, 32) if rnd == 0 else a("ee", 0, 8)
+        CW = a("ee", 8, 16)
         ts(a("cl"), a("acc"), 0.5, A.mult, 104.0, A.add)
         act(CW, a("acc"), scale=0.5, bias=104.0)
         reg("p", [mm(bank(7, 8, 16), I16, CW, False, False)])
@@ -415,85 +347,78 @@ def rank_program(g, core, T, topo):
         act(a("sv", 0, 8), a("acc"), F.Sign, 1.0, -191.0)
         act(qr, a("oh"), scale=RC)
         tt(qh, ind(a("hs"), a("cl")), a("oh"), A.mult)
-        wrap(bank(7, 0, 16), lambda r: qrow(1, 2, r), False)
+        wrap(bank(7, 0, 16), lambda r: qrow(0, 3, r, 2), False)
         tt(a("lw"), ind(a("low"), a("cl")), a("oh"), A.mult)
         act(a("crow"), ind(a("nrow"), a("cl")))
-        SV = a("sv", 8, 16)
+        act(ql, a("lw"), scale=float(LO))
+        act(a("sv", 8, 16), a("sv", 0, 8), scale=3712.0, bias=3712.0)
         if rnd == 0:
+            act(qm, a("lw"), scale=22.0)
             cp(a("rlw", 0, 512), a("rli"))
-            act(ql, a("lw"), scale=float(LO))
-            act(qp, a("oh"), scale=RRS)
-            act(SV, a("sv", 0, 8), scale=28.0, bias=28.0)
-        else:
-            act(qo, a("lw"), scale=float(V))
-            act(SV, a("sv", 0, 8), scale=3136.0, bias=3136.0)
+            act(a("sv", 16, 24), a("sv", 0, 8), scale=448.0, bias=448.0)
         reg("p", [mm(bank(4, 0, 128), a("blk"), qh, True, True)])
         cp(a("wl"), bank(7, 0, 16))
-        if rnd == 0:
-            reg("p", [mm(bank(6, 8, 32), I1, a("ee", 8, 32), True, False)])
-            wrap(bank(6, 8, 32), lambda r: qrow(1, 3, r), False, False)
-        else:
-            reg("p", [mm(bank(6, 0, 16), I1, a("ee", 0, 16), True, False)])
-            wrap(bank(6, 0, 16), lambda r: qrow(0, 2, r), False, False)
+        NL = 3 - rnd
+        reg("p", [mm(bank(6, 0, 8 * NL), I1, a("ee", 0, 8 * NL), True, False)])
+        rows = [(a("cs", 15 - r, 143 - r), qrow(0, NL, r)) for r in range(16)]
+        reg("p", grp(bank(6, 0, 8 * NL), rows[:10], False, False))
 
         cp(a("cu"), ind(a("rlw"), a("wl", 0, 8)))
-        if rnd == 1:
-            act(a("jq"), bank(4, 0, 128))
         act(a("wa"), ind(a("wv"), a("wl", 8, 16)))
         reg("p", [mm(bank(5, 300, 428), a("wa"), IN, True, True)])
+        reg("p", grp(bank(6, 0, 8 * NL), rows[10:], False, False))
         if rnd == 0:
             act(a("nb"), bank(7, 0, 8), scale=-262144.0, bias=67108864.0)
         else:
-            act(a("nb"), bank(7, 0, 8), bias=-256.0)
+            act(a("nc"), bank(7, 0, 8), bias=-256.0)
+            act(a("jq"), bank(4, 0, 128))
         act(a("wt"), bank(5, 300, 428), scale=SG)
-        if rnd == 0:
-            reg("p", [mm(bank(6, 16, 24), I16, CW, False, False), mm(bank(6, 16, 24), I16, SV, False, False), mm(bank(6, 24, 32), I1, SV, False, False)])
-        else:
-            reg("p", [mm(bank(6, 0, 8), I1, SV, False, False)])
+        reg("p", [mm(bank(6, 8, 16), I1, a("sv", 8, 16), False, False)]
+            + [mm(bank(6, 16, 24), l, r, False, False) for l, r in ((I16, CW), (I1, a("sv", 16, 24)))[:2 - 2 * rnd]])
         reg("p", [mm(bank(7, 0, 128), I1, a("krow"), True, False)])
         yc = [a("m1", YC + 512 * b, YC + 512 * b + 512) for b in range(4)]
         ab = [a("m1", AB + 512 * b, AB + 512 * b + 512) for b in range(4)]
-        src = [ind(a("mu", 0, W), a("cu", 32 * b, 32 * b + 32)) for b in range(4)]
+        src = [ind(a("yy"), a("cu", 32 * b, 32 * b + 32)) for b in range(4)]
         act(yc[0], src[0])
         cp(yc[2], src[2])
         act(yc[1], src[1])
         cp(yc[3], src[3])
-        for b in (0, 2, 1, 3):
+        for b in (2, 0, 3, 1):
             reg("p", [mm(bank(b, 0, 512), a("wt"), a("ex", 512 * b, 512 * b + 512), True, b >= 2)])
-            if b == 1:
+            if b == 3:
                 reg("p", [mm(bank(0, 0, 512), I1, yc[0], False, True)])
-        reg("p", grp(bank(5, 0, 128), [(a("blk"), qr), (a("blk"), a("crow"))]))
+        column = [(a("blk"), qr), (a("blk"), a("crow"))]
         reg("p", [mm(bank(1, 0, 512), I1, yc[1], False, True)])
         reg("p", [mm(bank(7, k, 128, 16), a("m1", YC + k, YC + 2048, 16), a("gn"), False, False) for k in range(16)])
+        reg("p", grp(bank(5, 0, 128), column))
         tt(ab[2], yc[2], bank(2, 0, 512), A.max)
         act(ab[0], bank(0, 0, 512), F.Relu)
         tt(ab[3], yc[3], bank(3, 0, 512), A.max)
         act(ab[1], bank(1, 0, 512), F.Relu)
         reg("p", [mm(bank(7, k, 128, 16), a("m1", AB + k, AB + 2048, 16), a("gp"), False, k == 15) for k in range(16)])
-        (cp, act)[rnd](a("cf"), ind(a("rlw"), a("wl", 0, 8)))
-        one, P1, P2 = bank(0, 0, 128), bank(2, 0, 128), bank(3, 0, 128)
+        act(a("cf"), ind(a("rlw"), a("wl", 0, 8)))
         if rnd == 0:
-            wrap(bank(6, 16, 32), lambda r: qrow(3, 2, r), False)
-            reg("p", grp(P1, [(top("d1", 2), top("half", 2)), (a("s1b"), qr), (a("s1b"), a("crow"))], True, False))
-            reg("p", grp(P2, [(top("d2", 1), top("half", 1)), (a("s2b"), qr), (a("s2b"), a("crow"))], True, False))
-        else:
-            wrap(bank(6, 0, 8), lambda r: qrow(2, 1, r), False, True, "cs2")
-            reg("p", grp(P2, [(a("s2b"), qr), (a("s2b"), a("crow"))], True, False))
-        HJ = a("hj") if rnd == 0 else bank(6, 8, 16)
+            act(a("junk", 1248, 1448), bank(4, 200, 400), acc=c1("thf", 2))
+        one, NEW = bank(0, 0, 128), bank(3, 0, 128)
+        wrap(bank(6, 8, 8 * NL), lambda r: qrow(2, NL - 1, r), False, True, "cs2")
+        reg("p", grp(NEW, column, True, False))
+        TURN = bank(2, 0, 128)
+        if rnd == 0:
+            reg("p", grp(TURN, [(r, l) for l, r in column], True, False))
+        HJ = a("hj") if rnd == 0 else bank(6, 0, 8)
         rhyme = [lambda: scan(a("dmn"), a("rsj"), a("dab"), A.add, A.min),
                  lambda HJ=HJ: tt(a("da"), HJ, a("dmn", 127, 1024, 128), A.subtract),
                  lambda: tt(a("db"), a("da"), a("dump"), A.min),
                  lambda: ts(a("dl"), a("db"), 256.0, A.add),
                  lambda: scatter(a("rlw"), a("dl"), a("tr"), a("cf"))]
         if rnd == 0:
-            reg("s", [actv(a("dab", 128 * t, 128 * t + 128), bank(4, 0, 128), F.Abs, 262144.0, c1("nb", t)) for t in range(8)])
             tt(a("vm"), bank(5, 0, 128), a("cf"), A.subtract)
-            first(1, 0, 0, 24)
+            act(a("ks"), bank(7, 0, 128))
             scan(a("km"), a("rsk"), bank(7, 0, 128), A.add, A.min)
-            cp(a("ks"), bank(7, 0, 128))
+            reg("s", [actv(a("dab", 128 * t, 128 * t + 128), bank(4, 0, 128), F.Abs, 262144.0, c1("nb", t)) for t in range(8)])
         else:
             for t in range(8):
-                ts(a("dab", 128 * t, 128 * t + 128), a("jq"), c1("nb", t), A.not_equal, 262144.0, A.mult)
+                ts(a("dab", 128 * t, 128 * t + 128), a("jq"), c1("nc", t), A.not_equal, 262144.0, A.mult)
             act(a("ks"), bank(7, 0, 128))
             rhyme[0]()
             scan(a("km"), a("rsk"), bank(7, 0, 128), A.add, A.min)
@@ -501,52 +426,48 @@ def rank_program(g, core, T, topo):
         tt(a("eq"), ind(a("km"), a("lsu")), a("ks"), A.is_equal)
         reg("p", [mm(one, a("eq"), I1, True, True)])
         if rnd == 0:
-            cp(a("sl", 16, 32), bank(6, 16, 32))
+            cp(a("sl"), bank(6, 8, 24))
         else:
             rhyme[1]()
-            cp(a("sl", 0, 8), bank(6, 0, 8))
+            cp(a("sl", 0, 8), bank(6, 8, 16))
             rhyme[2]()
         tt(a("tr"), one, a("vm"), A.mult)
+        reg("p", [mm(NEW, a("nb32"), a("tr"), False, True)])
         if rnd == 0:
-            reg("p", [mm(P1, a("l1m"), a("tr"), False, True)])
-        reg("p", [mm(P2, a("l2m"), a("tr"), False, True)])
+            reg("p", [mm(TURN, a("tr"), a("nb32"), False, True)])
+        act(a("val"), NEW)
         if rnd == 0:
+            first(1, 0, 0, 16)
+            scatter(a("ow"), a("sl", 0, 8), a("val"))
+            for tb in (0, 1):
+                dma("y", [(tab("pt", tb), owrows(tb))])
+            tt(a("cm"), TURN, a("dm"), A.mult)
+            reg("p", [mm(bank(1, 0, 8), a("cm"), a("g32"), True, True)])
+            aside(1, 0)
             act(a("xv"), ind(a("xa"), a("wl", 8, 16)))
-            first(1, 0, 24, 40)
-            ts(a("rr"), P1, MR, A.add, MR2, A.subtract)
-            tt(a("val"), P2, a("rr"), A.add)
-            scatter(a("wb"), a("sl", 24, 32), a("val"))
-            for nms in ((0, 1), (2,)):
-                for tb in (0, 1):
-                    dma("y", [(tab(("ft", "rt", "ht")[j], tb), wrow(j, tb)) for j in nms])
-            act(a("vb"), a("val"), scale=MK)
-            wrap(bank(1, 0, 8), lambda r: a("vb", r, 128, 16))
-            act(a("junk", 1248, 1448), bank(4, 200, 400), acc=c1("thf", 2))
+            act(a("hj"), bank(6, 0, 8))
             act(c1("thf", 3), c1("thf", 2), bias=-7.5)
             act(c1("thf", 4), c1("thf", 2), bias=c1("thf", 0))
+            aside(1, 1)
             act(c1("thf", 5), c1("thf", 3), bias=M16)
+            aside(1, 2)
             act(c1("thf", 6), c1("thf", 5), bias=-M16)
             act(c1("thf", 1), c1("thf", 6), scale=-1.0, bias=c1("thf", 4))
-            ghosts("xb", ("m1", 0), ("m1", ML), ("mu", 0))
-            act(a("hj"), bank(6, 8, 16))
-            first(1, 0, 40, 144)
-            ts(a("cc"), bank(1, 0, 8), -8.5, A.add)
-            place_mm(0)
+            ghosts("xb", *WINDOWS)
+            first(1, 0, 16, 64)
+            cp(a("cc"), bank(1, 0, 8))
+            first(1, 0, 64, OFF[1])
             tt(a("pv"), ind(a("xb"), a("cc")), a("xv"), A.max)
-            place(0)
-            first(1, 0, 144, 200)
-            place_mm(1)
-            for tb in (1, 0):
-                reg("p", grp(bank(4 + tb, 0, 200), [(I1, tab("ft", tb, 200)), (I1, tab("rt", tb, 200))]))
-            ts(a("l1", 200, 400), bank(5, 0, 200), -8.5, A.add)
-            scatter(a("m1", 0, LO + V), a("sl", 16, 24), a("pv"))
-            again(0, 0, 64)
-            again(0, 64, 200)
-            place(1)
-            first(1, 1, 0, 120, 0)
+            cp(tab("ln", 0), tab("pt", 0))
+            scatter(a("m1", 0, 4400 + V), a("sl", 8, 16), a("pv"))
+            cp(tab("ln", 1), tab("pt", 1))
+            act(a("ht"), a("pt"), bias=65792.5)
+            for lo, hi in ((0, 64), (64, 128), (128, 200)):
+                again(0, lo, hi)
+            first(1, 1, 0, 56, 0)
+            first(1, 1, 56, 120, 56)
             first(1, 1, 120, 200, 120)
         else:
-            act(a("val"), P2)
             rhyme[3]()
             rhyme[4]()
             dma("y", [(hbm(T.rl1[:], "out3"), a("rlw", 0, 512))])
@@ -565,7 +486,8 @@ def rank_program(g, core, T, topo):
             mask = (1 << pool.pop()) | (1 << pool.pop())
             rid, pid = topo.addr(dst)[0:2]
             trs.append(RemoteDMATransfer(dst_ids=[DstId(rid=rid, pnc=pid)], dma_engine_mask=mask, remote_sem=T.sem.arr,
-                                         src=T.sb[:, 128 * (d - 1):128 * d], dst=T.xb[:, V + 128 * (d - 1):V + 128 * d]))
+                                         srcs=[T.sb[:, o + 128 * (d - 1):o + 128 * d] for o in (0, W - V)],
+                                         dsts=[T.xb[:, V + 128 * (d - 1):V + 128 * d]], alu_op=2))
         g.remote_dma_fused(trs, local_sem=T.sem.sent)
 
     hist = {}

from concourse.bass import DstId, RemoteDMATransfer
from concourse.mybir import AluOpType, AxisListType, ActivationFunctionType

V, W, NR = 3200, 4096, 8
LO = 4352
SPEC = {
    "bfloat16": "xa 4096 xb 4096 wv 3328 m1 12800 m2 8192 mu 7552 yy 4096 ad 6400 ht 400 sb 1792 nrow 208 krow 128 jq 128 id1 128 idn 128 "
                "dm 128 jc 8 nc 8 i16 128 ones 128 blk 128 mt 128 cs 144 cs2 144 g1 8 gp 8 gn 8 ca 200 cd 200 c160 208 cw 16 ee 24 sv 24 rsk 128 rsj 1024 bad 208 low 208 "
                "sc 208 junk 1456 cmp 432 oh 128 wa 128 wt 128 xv 128 pv 128 crow 128 ex 2048 dab 1024 dmn 1024 eq 128 lw 128 hs 208",
    "float32": "pt 400 rlw 640 thf 8 col 16 jp 128 t16 8 jh 8 dump 8 id32 128 in32 128 nb32 128 g32 8 cm 128 ow 10632 tu 200 duc 200 kt 208 "
               "tm 200 acc 8 cf 128 vm 128 tr 128 nb 8 hj 8 da 8 db 8 km 128 ks 128 val 128",
    "int32": "ti 400 rli 512 sni 56 thi 4",
    "uint16": "l1 400 ln 400 snu 56 lsu 8 cl 8 wl 16 sl 16 cu 128 dl 8 cc 8",
}
SCRATCH = {"ps": ("psum", [128, 4096], "float32"), "qq": ("sbuf", [128, 4, 128], "bfloat16")}
for _d, _s in SPEC.items():
    _w = _s.split()
    for _i in range(0, len(_w), 2):
        SCRATCH[_w[_i]] = ("sbuf", [128, int(_w[_i + 1])], _d)
SEMAPHORES = ["ev", "es", "ep", "eg", "arr", "sent"] + ["d%d" % i for i in range(40)]

SEC = [(0, 0, 64), (0, 64, 128), (0, 128, 200), (1, 0, 56), (1, 56, 120), (1, 120, 176), (1, 176, 200)]
SLOT = [0, 1024, 2048, 3072, 4096, 5120, 6016, 6400]
OFF = (156, 148)
CUT, HOP = 120, (180, 172)
SBS = 32
REFILL, SUMS = {1: 3, 2: 4, 3: 5, 4: 6}, {1: 0, 3: 1, 4: 2, 5: 3, 6: 4}
M16 = 1.5 * 2.0 ** 27
HB = 66048
BIG = 1 << 23
ALL = 0xFFFF
YC, AB, ML = LO, LO + 2048, 2 * LO
FULL = 7


def rank_program(g, core, T, topo):
    rank = T.rank_of(core)
    if rank is None:
        return
    A, F = AluOpType, ActivationFunctionType
    ve, se, pe = g.vector, g.scalar, g.tensor
    queue = {"v": ve, "s": se, "p": pe, "g": g, "y": g.sync}
    ops = []

    def a(name, lo=0, hi=None, st=1):
        hi = SCRATCH[name][1][1] if hi is None else hi
        return (T[name][:, lo:hi:st] if st > 1 else T[name][:, lo:hi], [(name, lo, hi, ALL)])

    def part(name, j, lo, hi):
        return (T[name][j:128:16, lo:hi], [(name, lo, hi, 1 << j)])

    def c1(name, i):
        return a(name, i, i + 1)

    def hbm(t, key=None):
        return (t, [(key, 0, 1, ALL)] if key else [])

    def bank(b, lo, hi, st=1):
        return a("ps", 512 * b + lo, 512 * b + hi, st)

    def qrow(i, n=1, r=None, st=1):
        ap = T.qq[:, i, :] if r is None else T.qq[:, i:i + n:st, r:128:16]
        return (ap, [("qq", 128 * j, 128 * j + 128, ALL) for j in range(i, i + n, st)])

    def ind(w_, o):
        return (w_[0].indirect(o[0]), w_[1] + o[1])

    def val(x):
        return x[0] if isinstance(x, tuple) else x

    def rng(*xs):
        return [r for x in xs if isinstance(x, tuple) for r in x[1]]

    def reg(e, calls, kind="c"):
        ops.append({"e": e, "f": [c[0] for c in calls], "r": rng(*[x for c in calls for x in c[1]]),
                    "w": rng(*[x for c in calls for x in c[2]]), "k": kind})

    def ts(o, i, s1, o0, s2=None, o1=None):
        if o1 is None:
            reg("v", [(lambda: ve.tensor_scalar(o[0], i[0], val(s1), None, o0), [i, s1], [o])])
        else:
            reg("v", [(lambda: ve.tensor_scalar(o[0], i[0], val(s1), val(s2), o0, o1), [i, s1, s2], [o])])

    def tt(o, i, j, op):
        reg("v", [(lambda: ve.tensor_tensor(o[0], i[0], j[0], op), [i, j], [o])])

    def cpv(o, i):
        return (lambda: ve.tensor_copy(o[0], i[0]), [i], [o])

    def cp(o, i):
        reg("v", [cpv(o, i)])

    def scatter(w_, o, i, j=None):
        out = w_[0].indirect(o[0])
        if j is None:
            reg("v", [(lambda: ve.tensor_copy(out, i[0]), [i, o], [w_])])
        else:
            reg("v", [(lambda: ve.tensor_tensor(out, i[0], j[0], A.add), [i, j, o], [w_])])

    def scan(o, d0, d1, o0, o1):
        reg("v", [(lambda: ve.tensor_tensor_scan(o[0], d0[0], d1[0], 0.0, o0, o1), [d0, d1], [o])])

    def red(o, i):
        reg("v", [(lambda: ve.tensor_reduce(o[0], i[0], AxisListType.X, A.add), [i], [o])])

    def mset(o, c):
        reg("v", [(lambda: ve.memset(o[0], c), [], [o])])

    def actv(o, i, f=F.Identity, scale=1.0, bias=0.0, acc=None):
        if acc is None:
            return (lambda: se.activation(o[0], i[0], f, bias=val(bias), scale=val(scale)), [i, scale, bias], [o])
        return (lambda: se.activation(o[0], i[0], f, bias=val(bias), scale=val(scale), accum_out=acc[0]), [i, scale, bias], [o, acc])

    def act(*x, **k):
        reg("s", [actv(*x, **k)])

    def mm(o, l, r, s0, s1):
        return (lambda: pe.matmul(o[0], l[0], r[0], s0, s1), [l, r], [o])

    def grp(o, terms, s0=True, s1=True):
        return [mm(o, l, r, s0 and i == 0, s1 and i == len(terms) - 1) for i, (l, r) in enumerate(terms)]

    def wrap(o, src, s0=True, s1=True, by="cs"):
        reg("p", grp(o, [(a(by, 15 - r, 143 - r), src(r)) for r in range(16)], s0, s1))

    def iota(o, pat, base=0, cm=0):
        reg("g", [(lambda: g.iota(o[0], pat, base, cm, allow_small_or_imprecise_dtypes=True), [], [o])])

    def fill(o, n, v):
        iota(o, [[0, n]], v)

    def sel(o, i, pat, op, fl, base, cm):
        reg("g", [(lambda: g.affine_select(o[0], i[0], pat, op, fl, base, cm), [i], [o])])

    def dma(e, pairs):
        reg(e, [((o[0], i[0]), [i], [o]) for o, i in pairs], "d")

    PF, RC, UP, DOWN, SG = [c1("col", i) for i in range(5)]
    tmp = [c1("col", i) for i in range(8, 12)]
    I1, IN, I16 = a("id1"), a("idn"), a("i16")
    qh, ql, qr, qm = [qrow(i) for i in range(4)]
    nr = a("nrow", 0, 128)

    def tab(nm, tb, lo=0, hi=200):
        return a(nm, 200 * tb + lo, 200 * tb + hi)

    def owrows(tb):
        return part("ow", FULL, LO * tb, LO * tb + V)

    def classes():
        reg("p", grp(bank(7, 256, 456), [(a("id32"), tab("pt", 1)), (a("in32"), tab("pt", 0)), (I1, tab("ht", 0)), (IN, tab("ht", 1))])
            + grp(bank(6, 256, 456), [(a("id32"), tab("pt", 0)), (IN, tab("ht", 0)), (I1, a("ca")), (I1, a("cd"))]))

    def ghosts(src, *to):
        for nm, o in to:
            sel(a(nm, o + V, o + W), a(src, V, W), [[0, W - V]], A.is_ge, 0.0, 0, 0)

    WINDOWS = (("m1", 0), ("m2", 0), ("m1", ML), ("m2", W), ("yy", 0))

    dma("y", [(tab("ti", 0), hbm(T.up[:])), (tab("ti", 1), hbm(T.lo[:]))])
    dma("y", [(a("xa", 0, 2048), hbm(T.x[:, 0:2048]))])
    dma("y", [(a("xa", 2048, W), hbm(T.x[:, 2048:W]))])
    dma("y", [(a("xb", 2048, V), hbm(T.x[:, 2048:V]))])
    dma("y", [(a("wv", 0, V), hbm(T.w[:]))])
    glo, ghi = ([[-16, 8]], A.is_ge, 0.0, 0, 1), ([[16, 8]], A.is_ge, 0.0, 15, -1)
    blo, bhi = ([[-16, 8], [0, 16]], A.is_ge, 0.0, 0, 1), ([[16, 8], [0, 16]], A.is_ge, 0.0, 15, -1)
    diag = [[-1, 128]]
    iota(PF, [[0, 1]], 0, 1)
    iota(a("nrow"), [[1, 208]])
    iota(a("t16"), [[16, 8]])
    for nm, n, v in (("ones", 128, 1), ("cs", 144, 0), ("mt", 128, -1)):
        fill(a(nm), n, v)
    sel(a("g1"), a("ones", 0, 8), *glo)
    sel(a("blk"), a("ones"), *blo)
    sel(a("cs", 15, 128, 16), a("g1"), *ghi)
    sel(a("blk"), a("blk"), *bhi)
    sel(a("mt"), a("mt"), *bhi)
    fill(a("ca"), 200, -256)
    sel(a("mt"), a("mt"), diag, A.is_gt, 0.0, 0, 1)
    fill(a("cd"), 200, HB)
    sel(a("mt"), a("mt"), diag, A.not_equal, 256.0, 0, 1)
    iota(a("krow"), [[0, 8], [1, 16]])
    iota(a("jp"), [[1, 128]], 257)
    ghosts("xa", *WINDOWS)
    for nm, lo, n, v in (("c160", 0, 208, 160), ("wv", V, 128, 0), ("rlw", 512, 128, 0), ("m1", W, LO - W, 0), ("cw", 0, 8, 256), ("cw", 8, 8, 0),
                         ("ee", 16, 8, 0), ("bad", 200, 8, 1), ("low", 200, 8, 0), ("hs", 200, 8, 256), ("cmp", 208, 8, -26), ("cmp", 424, 8, -26)):
        fill(a(nm, lo, lo + n), n, v)
    for nm, v, st in (("rsj", -1024.0, 128), ("rsk", 0.0, 16)):
        mset(a(nm), v)
        mset(a(nm, 0, None, st), float(BIG))
    ts(IN, nr, PF, A.is_equal, -1.0, A.mult)
    ts(I1, nr, PF, A.is_equal)
    ts(a("lsu"), a("t16"), 15.0, A.add)
    reg("v", [cpv(a("ex", k, 2048, 16), I1) for k in range(16)])
    cp(a("l1"), a("ti"))
    cp(a("pt"), a("ti"))
    cp(a("xb", 0, 2048), a("xa", 0, 2048))
    act(tmp[0], PF, bias=-7.5)
    act(tmp[1], tmp[0], bias=M16)
    act(tmp[2], tmp[1], bias=-M16)
    act(RC, tmp[2], scale=-1.0, bias=PF)
    act(SG, PF, F.Sign, -1.0, 63.5)
    act(tmp[3], RC, F.Sign, -1.0, 7.5)
    act(a("jc"), a("t16"), bias=RC)
    act(UP, tmp[3], F.Relu)
    act(DOWN, tmp[3], F.Relu, -1.0)
    act(a("jh"), a("jc"), bias=0.5)
    act(a("ee", 0, 8), a("jc"), scale=1024.0, bias=-127 * 1024.0)
    act(a("dump"), a("jc"), bias=256.0)
    for nm, src, sc in (("i16", I1, 16.0), ("id32", I1, 1.0), ("in32", I1, -1.0), ("gn", a("cs", 15, 128, 16), -16.0), ("gp", a("cs", 15, 128, 16), 32.0),
                        ("cs2", a("cs"), 200.0), ("g32", a("cs", 15, 128, 16), 1.0), ("nb32", a("blk"), -1.0)):
        act(a(nm), src, scale=sc)
    act(a("ht"), a("pt"), bias=65792.5)
    classes()

    def first(rnd, tb, lo, hi, cut=None):
        xn, xo = ("xa", "xb") if rnd == 0 else ("xb", "xa")
        tt(a("m1", ML * tb + 16 * lo, ML * tb + 16 * hi), ind(a(xn), tab(("l1", "ln")[rnd * tb], tb, lo, hi)), a(xo, 16 * lo, 16 * hi), A.max)
        if cut is not None:
            again(tb, cut, hi)

    def again(tb, lo, hi):
        dma("y", [(a("mu", LO * tb + 16 * lo, LO * tb + 16 * hi), a("m1", ML * tb + 16 * lo, ML * tb + 16 * hi))])

    def aside(rnd, step):
        c0, h = 16 * OFF[rnd], 8 * (200 - OFF[rnd])
        G, R = [[a("ad", o + h * j, o + h * j + h) for j in (0, 1)] for o in (0, 1024)]
        D, S = [[bank(b + j, 0, h) for j in (0, 1)] for b in (4, 2)]
        if step == 0:
            act(a("ad", 0, 2 * h), ind(a(("xa", "xb")[rnd]), tab("l1", 0, OFF[rnd], 200)))
            for j in (0, 1):
                reg("p", grp(D[j], [(I1, a("xa", c0 + h * j, c0 + h * j + h)), (IN, G[j])]))
            reg("p", [mm(S[j], I1, G[j], True, False) for j in (0, 1)])
        for j in (0, 1):
            if step == 1:
                act(R[j], D[j], F.Relu)
                reg("p", [mm(S[j], I1, R[j], False, True)])
            elif step == 2:
                act(a("m1", c0 + h * j, c0 + h * j + h), S[j])

    def hop(rnd, tb, lo, hi, by=act):
        by(a("m2", W * tb + 16 * lo, W * tb + 16 * hi), ind(a("m1", ML * tb, ML * tb + W), tab(("l1", "ln")[rnd], tb, lo, hi)))

    def cuts(i):
        out, x = [], SLOT[i]
        while x < SLOT[i + 1]:
            z = min(SLOT[i + 1], x + 512 - (x - SLOT[i]) % 512, V if x < V else 2 * V)
            out.append((1024 * (i % 3) + x - SLOT[i], x, z - x))
            x = z
        return out

    def minus_w(i):
        reg("p", [mm(a("ps", o, o + n), IN, a("wv", x % V, x % V + n), o % 512 == 0, False) for o, x, n in cuts(i)])

    def second(rnd, i):
        tb, lo, hi = SEC[i]
        o = a("mu", LO * tb + 16 * lo, LO * tb + 16 * hi)
        tt(o, ind(a("m2", W * tb, W * tb + W), tab(("l1", "ln")[rnd], tb, lo, hi)), o, A.max)

    def plus_m(i):
        cs_ = cuts(i)
        reg("p", [mm(a("ps", o, o + n), I1, a("mu", x + (LO - V) * (x // V), x + (LO - V) * (x // V) + n), False,
                     j == len(cs_) - 1 or cs_[j + 1][0] % 512 == 0) for j, (o, x, n) in enumerate(cs_)])

    def absd(i):
        act(a("ad", SLOT[i], SLOT[i + 1]), a("ps", 1024 * (i % 3), 1024 * (i % 3) + SLOT[i + 1] - SLOT[i]), F.Abs)

    def dist(i):
        tb, lo, hi = SEC[i] if i < 5 else (1, SEC[5][1], 200)
        wrap(bank(7 - tb, lo, hi), lambda r: a("ad", V * tb + 16 * lo + r, V * tb + 16 * hi, 16))

    def halves(tb, lo, hi):
        dma("y", [(part("yy", j, lo, hi), part("mu", j, LO * tb + lo, LO * tb + hi)) for j in range(8 * tb, 8 * tb + 8)])

    first(0, 0, 0, 128, 0)
    for step in range(3):
        aside(0, step)
    first(0, 0, 128, OFF[0])
    again(0, 128, 200)
    first(0, 1, 0, 120, 0)
    dma("y", [(c1("thi", 0), hbm(T.th[:])), (a("sni"), hbm(T.snd[:]))])
    first(0, 1, 120, 200, 120)
    dma("y", [(a("rli"), hbm(T.rl[:]))] + [(owrows(tb), tab("pt", tb)) for tb in (0, 1)])

    for rnd in range(2):
        hop(rnd, 0, 0, 200)
        hop(rnd, 1, 0, CUT)
        for i in range(3):
            minus_w(i)
        if rnd == 1:
            classes()
        for i in range(7):
            if (rnd, i) == (0, 4):
                cp(a("snu"), a("sni"))
                act(a("sb", 896, 896 + 16 * SBS), ind(a("mu", 0, V), a("snu", 0, SBS)), scale=UP)
            if (rnd, i) == (0, 5):
                cp(c1("thf", 0), c1("thi", 0))
            if i == 3:
                hop(rnd, 1, HOP[rnd], 200, cp)
            second(rnd, i)
            plus_m(i)
            absd(i)
            if i == 0:
                hop(rnd, 1, CUT, HOP[rnd])
            if i in REFILL:
                minus_w(REFILL[i])
            if i in SUMS:
                dist(SUMS[i])
            if i == 6:
                act(a("tu"), bank(7, 0, 200), scale=-1.0, bias=c1("thf", rnd))
                act(a("duc"), bank(7, 0, 200))
            if i in (2, 6):
                halves(i // 6, 0, V)
        dist(5)
        if rnd == 0:
            ts(a("sb", 0, 896), ind(a("mu", LO, LO + V), a("snu")), DOWN, A.mult)
            ts(a("sb", 896 + 16 * SBS, 1792), ind(a("mu", 0, V), a("snu", SBS, 56)), UP, A.mult)
            reg("g", [(None, [a("sb")], [])], "x")
            ts(a("dm"), a("krow"), RC, A.is_equal)
            reg("y", [(None, [], [a("xb", V, W)])], "a")
        else:
            dma("y", [(hbm(T.y[:], "out0"), a("yy", 0, V))])
            for f in rhyme:
                f()

        tt(a("bad", 0, 200), bank(6, 0, 200), a("tu"), A.is_gt)
        reg("p", [mm(bank(0, 0, 208), a("blk"), a("bad"), True, True)])
        reg("p", [mm(bank(1, 0, 208), a("mt"), a("bad"), True, True)])
        tt(a("low", 0, 200), bank(6, 0, 200), a("duc"), A.is_gt)
        scan(a("sc"), bank(0, 0, 208), a("c160"), A.add, A.min)
        if rnd == 0:
            reg("p", [mm(bank(4, 200, 400), a("ones"), a("bad", 0, 200), True, True)])
        reg("s", [actv(a("junk", 208 * t, 208 * t + 208), a("sc"), F.Sign, -1.0, c1("jh", t), c1("acc", t)) for t in range(6)])
        tt(a("tm"), bank(7, 256, 456), a("low", 0, 200), A.mult)
        ts(a("cmp", 0, 208), a("sc"), c1("jc", 6), A.is_le, 2.0, A.mult)
        ts(a("cmp", 216, 424), a("sc"), c1("jc", 7), A.is_le, 2.0, A.mult)
        tt(a("kt"), bank(1, 0, 208), a("sc"), A.add)
        red(c1("acc", 6), a("cmp", 0, 216))
        red(c1("acc", 7), a("cmp", 216, 432))
        tt(a("hs", 0, 200), bank(6, 256, 456), a("tm"), A.add)
        reg("p", [mm(bank(7, 0, 16), I1, a("cw"), True, False)])
        CW = a("ee", 8, 16)
        ts(a("cl"), a("acc"), 0.5, A.mult, 104.0, A.add)
        act(CW, a("acc"), scale=0.5, bias=104.0)
        reg("p", [mm(bank(7, 8, 16), I16, CW, False, False)])
        tt(a("oh"), ind(a("kt"), a("cl")), a("jp"), A.is_equal)
        act(a("sv", 0, 8), a("acc"), F.Sign, 1.0, -191.0)
        act(qr, a("oh"), scale=RC)
        tt(qh, ind(a("hs"), a("cl")), a("oh"), A.mult)
        wrap(bank(7, 0, 16), lambda r: qrow(0, 3, r, 2), False)
        tt(a("lw"), ind(a("low"), a("cl")), a("oh"), A.mult)
        act(a("crow"), ind(a("nrow"), a("cl")))
        act(ql, a("lw"), scale=float(LO))
        act(a("sv", 8, 16), a("sv", 0, 8), scale=3712.0, bias=3712.0)
        if rnd == 0:
            act(qm, a("lw"), scale=22.0)
            cp(a("rlw", 0, 512), a("rli"))
            act(a("sv", 16, 24), a("sv", 0, 8), scale=448.0, bias=448.0)
        reg("p", [mm(bank(4, 0, 128), a("blk"), qh, True, True)])
        cp(a("wl"), bank(7, 0, 16))
        NL = 3 - rnd
        reg("p", [mm(bank(6, 0, 8 * NL), I1, a("ee", 0, 8 * NL), True, False)])
        rows = [(a("cs", 15 - r, 143 - r), qrow(0, NL, r)) for r in range(16)]
        reg("p", grp(bank(6, 0, 8 * NL), rows[:10], False, False))

        cp(a("cu"), ind(a("rlw"), a("wl", 0, 8)))
        act(a("wa"), ind(a("wv"), a("wl", 8, 16)))
        reg("p", [mm(bank(5, 300, 428), a("wa"), IN, True, True)])
        reg("p", grp(bank(6, 0, 8 * NL), rows[10:], False, False))
        if rnd == 0:
            act(a("nb"), bank(7, 0, 8), scale=-262144.0, bias=67108864.0)
        else:
            act(a("nc"), bank(7, 0, 8), bias=-256.0)
            act(a("jq"), bank(4, 0, 128))
        act(a("wt"), bank(5, 300, 428), scale=SG)
        reg("p", [mm(bank(6, 8, 16), I1, a("sv", 8, 16), False, False)]
            + [mm(bank(6, 16, 24), l, r, False, False) for l, r in ((I16, CW), (I1, a("sv", 16, 24)))[:2 - 2 * rnd]])
        reg("p", [mm(bank(7, 0, 128), I1, a("krow"), True, False)])
        yc = [a("m1", YC + 512 * b, YC + 512 * b + 512) for b in range(4)]
        ab = [a("m1", AB + 512 * b, AB + 512 * b + 512) for b in range(4)]
        src = [ind(a("yy"), a("cu", 32 * b, 32 * b + 32)) for b in range(4)]
        act(yc[0], src[0])
        cp(yc[2], src[2])
        act(yc[1], src[1])
        cp(yc[3], src[3])
        for b in (2, 0, 3, 1):
            reg("p", [mm(bank(b, 0, 512), a("wt"), a("ex", 512 * b, 512 * b + 512), True, b >= 2)])
            if b == 3:
                reg("p", [mm(bank(0, 0, 512), I1, yc[0], False, True)])
        column = [(a("blk"), qr), (a("blk"), a("crow"))]
        reg("p", [mm(bank(1, 0, 512), I1, yc[1], False, True)])
        reg("p", [mm(bank(7, k, 128, 16), a("m1", YC + k, YC + 2048, 16), a("gn"), False, False) for k in range(16)])
        reg("p", grp(bank(5, 0, 128), column))
        tt(ab[2], yc[2], bank(2, 0, 512), A.max)
        act(ab[0], bank(0, 0, 512), F.Relu)
        tt(ab[3], yc[3], bank(3, 0, 512), A.max)
        act(ab[1], bank(1, 0, 512), F.Relu)
        reg("p", [mm(bank(7, k, 128, 16), a("m1", AB + k, AB + 2048, 16), a("gp"), False, k == 15) for k in range(16)])
        act(a("cf"), ind(a("rlw"), a("wl", 0, 8)))
        if rnd == 0:
            act(a("junk", 1248, 1448), bank(4, 200, 400), acc=c1("thf", 2))
        one, NEW = bank(0, 0, 128), bank(3, 0, 128)
        wrap(bank(6, 8, 8 * NL), lambda r: qrow(2, NL - 1, r), False, True, "cs2")
        reg("p", grp(NEW, column, True, False))
        TURN = bank(2, 0, 128)
        if rnd == 0:
            reg("p", grp(TURN, [(r, l) for l, r in column], True, False))
        HJ = a("hj") if rnd == 0 else bank(6, 0, 8)
        rhyme = [lambda: scan(a("dmn"), a("rsj"), a("dab"), A.add, A.min),
                 lambda HJ=HJ: tt(a("da"), HJ, a("dmn", 127, 1024, 128), A.subtract),
                 lambda: tt(a("db"), a("da"), a("dump"), A.min),
                 lambda: ts(a("dl"), a("db"), 256.0, A.add),
                 lambda: scatter(a("rlw"), a("dl"), a("tr"), a("cf"))]
        if rnd == 0:
            tt(a("vm"), bank(5, 0, 128), a("cf"), A.subtract)
            act(a("ks"), bank(7, 0, 128))
            scan(a("km"), a("rsk"), bank(7, 0, 128), A.add, A.min)
            reg("s", [actv(a("dab", 128 * t, 128 * t + 128), bank(4, 0, 128), F.Abs, 262144.0, c1("nb", t)) for t in range(8)])
        else:
            for t in range(8):
                ts(a("dab", 128 * t, 128 * t + 128), a("jq"), c1("nc", t), A.not_equal, 262144.0, A.mult)
            act(a("ks"), bank(7, 0, 128))
            rhyme[0]()
            scan(a("km"), a("rsk"), bank(7, 0, 128), A.add, A.min)
            tt(a("vm"), bank(5, 0, 128), a("cf"), A.subtract)
        tt(a("eq"), ind(a("km"), a("lsu")), a("ks"), A.is_equal)
        reg("p", [mm(one, a("eq"), I1, True, True)])
        if rnd == 0:
            cp(a("sl"), bank(6, 8, 24))
        else:
            rhyme[1]()
            cp(a("sl", 0, 8), bank(6, 8, 16))
            rhyme[2]()
        tt(a("tr"), one, a("vm"), A.mult)
        reg("p", [mm(NEW, a("nb32"), a("tr"), False, True)])
        if rnd == 0:
            reg("p", [mm(TURN, a("tr"), a("nb32"), False, True)])
        act(a("val"), NEW)
        if rnd == 0:
            first(1, 0, 0, 16)
            scatter(a("ow"), a("sl", 0, 8), a("val"))
            for tb in (0, 1):
                dma("y", [(tab("pt", tb), owrows(tb))])
            tt(a("cm"), TURN, a("dm"), A.mult)
            reg("p", [mm(bank(1, 0, 8), a("cm"), a("g32"), True, True)])
            aside(1, 0)
            act(a("xv"), ind(a("xa"), a("wl", 8, 16)))
            act(a("hj"), bank(6, 0, 8))
            act(c1("thf", 3), c1("thf", 2), bias=-7.5)
            act(c1("thf", 4), c1("thf", 2), bias=c1("thf", 0))
            aside(1, 1)
            act(c1("thf", 5), c1("thf", 3), bias=M16)
            aside(1, 2)
            act(c1("thf", 6), c1("thf", 5), bias=-M16)
            act(c1("thf", 1), c1("thf", 6), scale=-1.0, bias=c1("thf", 4))
            ghosts("xb", *WINDOWS)
            first(1, 0, 16, 64)
            cp(a("cc"), bank(1, 0, 8))
            first(1, 0, 64, OFF[1])
            tt(a("pv"), ind(a("xb"), a("cc")), a("xv"), A.max)
            cp(tab("ln", 0), tab("pt", 0))
            scatter(a("m1", 0, 4400 + V), a("sl", 8, 16), a("pv"))
            cp(tab("ln", 1), tab("pt", 1))
            act(a("ht"), a("pt"), bias=65792.5)
            for lo, hi in ((0, 64), (64, 128), (128, 200)):
                again(0, lo, hi)
            first(1, 1, 0, 56, 0)
            first(1, 1, 56, 120, 56)
            first(1, 1, 120, 200, 120)
        else:
            rhyme[3]()
            rhyme[4]()
            dma("y", [(hbm(T.rl1[:], "out3"), a("rlw", 0, 512))])
            scatter(a("ow"), a("sl", 0, 8), a("val"))
            dma("s", [(hbm(T.up1[:], "out1"), owrows(0)), (hbm(T.lo1[:], "out2"), owrows(1))])
    reg("y", [(None, [hbm(None, "out%d" % i) for i in range(4)], [])], "n")
    reg("g", [(None, [], [])], "e")

    def exchange():
        eng = topo.engines(core, T.cores[(rank + 1) % NR])
        far, near = list(eng[0::2]), list(eng[1::2])
        trs = []
        for d in range(1, NR):
            dst = T.cores[(rank + d) % NR]
            pool = far if topo.die(dst) != topo.die(core) else near
            mask = (1 << pool.pop()) | (1 << pool.pop())
            rid, pid = topo.addr(dst)[0:2]
            trs.append(RemoteDMATransfer(dst_ids=[DstId(rid=rid, pnc=pid)], dma_engine_mask=mask, remote_sem=T.sem.arr,
                                         srcs=[T.sb[:, o + 128 * (d - 1):o + 128 * d] for o in (0, W - V)],
                                         dsts=[T.xb[:, V + 128 * (d - 1):V + 128 * d]], alu_op=2))
        g.remote_dma_fused(trs, local_sem=T.sem.sent)

    hist = {}
    know = {e: {} for e in queue}
    for i, o in enumerate(ops):
        e = o["e"]
        use = [(r, False) for r in o["r"]] + [(r, True) for r in o["w"]]
        use = [((nm, lo // 512 * 512, -(-hi // 512) * 512, pm), wr) if nm == "ps" else ((nm, lo, hi, pm), wr) for (nm, lo, hi, pm), wr in use]
        need = {}
        for (nm, lo, hi, pm), wr in use:
            for l2, h2, p2, w2, j in hist.get(nm, []):
                src = ops[j]["src"]
                if l2 < hi and lo < h2 and pm & p2 and ((src != e) if nm == "ps" else (wr or w2)) and not (src == "p" and e == "p"):
                    need[src] = max(need.get(src, -1), j)
        o["waits"] = []
        for src, j in sorted(need.items(), key=lambda t: -t[1]):
            if know[e].get(src, -1) < j:
                o["waits"].append(j)
                ops[j]["inc"] = True
                for s2, j2 in list(ops[j]["know"].items()) + [(src, j)]:
                    know[e][s2] = max(know[e].get(s2, -1), j2)
        o["src"] = e if o["k"] == "c" else "z%d" % i
        o["know"] = dict(know[e]) if o["k"] != "a" else {}
        for (nm, lo, hi, pm), wr in use:
            hist.setdefault(nm, []).append((lo, hi, pm, wr, i))
    count = {e: 0 for e in queue}
    nd = 0
    for o in ops:
        e, q = o["e"], queue[o["e"]]
        for j in o["waits"]:
            q.wait_ge(*ops[j]["sig"])
        if o["k"] == "c":
            ins = [f() for f in o["f"]][-1]
            if o.get("inc"):
                count[e] += 1
                ins.then_inc(T.sem["e" + e], 1)
                o["sig"] = (T.sem["e" + e], count[e])
        elif o["k"] == "d":
            sem = T.sem["d%d" % nd]
            nd += 1
            for dst, src in o["f"]:
                q.dma_start(dst, src).then_inc(sem, 16)
            o["sig"] = (sem, 16 * len(o["f"]))
        elif o["k"] == "a":
            o["sig"] = (T.sem.arr, 2 * (NR - 1))
        elif o["k"] == "x":
            exchange()
        elif o["k"] == "e":
            g.wait_ge(T.sem.sent, 2 * (NR - 1))
